import numpy as np
import ml_dtypes


def mxq(x, axis, fmt="e4m3"):
    dtype, down = {"e4m3": (ml_dtypes.float8_e4m3fn, 7), "e5m2": (ml_dtypes.float8_e5m2, 14)}[fmt]
    v = np.moveaxis(np.asarray(x, np.float32).astype(ml_dtypes.bfloat16).astype(np.float64), axis, -1)
    blocks = v.reshape(v.shape[:-1] + (-1, 32))
    amax = np.abs(blocks).max(-1, keepdims=True)
    byte = np.maximum(np.where(amax > 0, np.frexp(amax)[1] - 1 + 127, 0) - down, 1)
    scale = np.exp2(byte - 127.0)
    codes = (blocks / scale).astype(np.float32).astype(dtype).astype(np.float64)
    return np.moveaxis((codes * scale).reshape(v.shape), -1, axis)


WIDE = False


def mx_kscale(k):
    if not WIDE:
        return np.ones(k)
    levels = np.array([10, -10, 5, -5, 0])
    if k % 512:
        return np.exp2(np.random.permutation(np.resize(levels, k // 32))).repeat(32)
    a = np.empty((k // 512, 16))
    for p in range(k // 512):
        a[p, :8] = np.random.permutation(np.resize(levels, 8))
        for g in range(8):
            far = levels[np.abs(levels - a[p, g]) >= 10]
            a[p, g + 8] = far[np.random.randint(len(far))]
    return np.exp2(a.ravel()).repeat(32)


def f64(x):
    return np.asarray(x).astype(np.float64)


def striped(idx):
    return np.tile(idx.reshape(-1, 16).T, (8, 1)).astype(np.uint16)


def unstriped(offs):
    return offs[:16].T.reshape(-1).astype(np.int64)


E2M1 = np.array([0.0, 0.5, 1.0, 1.5, 2.0, 3.0, 4.0, 6.0, -0.0, -0.5, -1.0, -1.5, -2.0, -3.0, -4.0, -6.0])


def pack_weight(w, fmt):
    k, n = w.shape
    w = f64(np.asarray(w, np.float32).astype(ml_dtypes.bfloat16)).reshape(k // 32, 32, n)
    amax = np.abs(w).max(1)
    if fmt == "e4m3":
        byte = np.frexp(amax)[1] - 1 + 127 - 7
    else:
        mant, ex = np.frexp(amax / 6.0)
        byte = np.where(mant > 0.5, ex, ex - 1) + 127
    byte = np.clip(np.where(amax > 0, byte, 1), 1, 254)
    scaled = (w * np.exp2(127.0 - byte)[:, None, :]).reshape(k, n).astype(np.float32)
    by_word = np.ascontiguousarray(scaled.reshape(k // 512, 128, 4, n).transpose(0, 1, 3, 2))
    if fmt == "e4m3":
        words = by_word.astype(ml_dtypes.float8_e4m3fn).view(np.uint8)
    else:
        c = by_word.astype(ml_dtypes.float4_e2m1fn).view(np.uint8) & 0xF
        words = (c[..., 0::2] | (c[..., 1::2] << 4)).reshape(k // 512, 128, 2 * n)
    return np.ascontiguousarray(words), np.ascontiguousarray(byte.astype(np.uint8).reshape(k // 512, 16, n))


def unpack_weight(words, scales, fmt):
    g, _, n = scales.shape
    words = np.ascontiguousarray(words).reshape(g, 128, n, -1)
    if fmt == "e4m3":
        vals = words.view(ml_dtypes.float8_e4m3fn).astype(np.float64)
    else:
        nib = np.empty((g, 128, n, 4), np.uint8)
        nib[..., 0::2] = words & 0xF
        nib[..., 1::2] = words >> 4
        vals = E2M1[nib]
    vals = vals * np.repeat(np.exp2(scales.astype(np.float64) - 127.0), 8, axis=1)[..., None]
    return vals.transpose(0, 1, 3, 2).reshape(g * 512, n)


def gelu(v):
    return 0.5 * v * (1.0 + np.tanh(np.sqrt(2.0 / np.pi) * (v + 0.044715 * v**3)))


def bf(x):
    return np.asarray(x, np.float32).astype(ml_dtypes.bfloat16)


def planes(Y):
    n, m = Y.shape
    b = f64(bf(Y)).reshape(n // 32, 32, m)
    amax = np.abs(b).max(1)
    byte = np.clip(np.where(amax > 0, np.frexp(amax)[1] - 1 + 127 - 7, 1), 1, 254)
    codes = (b * np.exp2(127.0 - byte)[:, None, :]).reshape(n, m).astype(np.float32).astype(ml_dtypes.float8_e4m3fn).view(np.uint8)
    words = codes.reshape(n // 512, 128, 4, m).transpose(0, 1, 3, 2)
    return np.ascontiguousarray(words), np.ascontiguousarray(byte.astype(np.uint8).reshape(n // 512, 16, m))


K, KA, KB, H, N, T, S, P = 1536, 512, 1024, 1024, 512, 2048, 1024, 512

def setup_inputs():
    n = np.random.standard_normal
    s = mx_kscale(K)[:, None]
    u = mx_kscale(H)[:, None]
    tab_words, tab_scales = pack_weight(n((K, T)) * s, "e4m3")
    w4_words, w4_scales = pack_weight(n((KB, H)) / np.sqrt(K) / s[KA:], "e2m1")
    w8_words, w8_scales = pack_weight(n((H, N)) / np.sqrt(H) / u, "e4m3")
    wa = n((H, N)) / np.sqrt(H) / u * np.exp(0.8 * n(N))[None, :]
    return {
        "tab_words": tab_words, "tab_scales": tab_scales,
        "offs": striped(np.random.permutation(T)[:S]),
        "pos1": striped(np.random.permutation(S)[:P]),
        "pos2": striped(np.random.permutation(S)[:P]),
        "w1": (n((KA, H)) / np.sqrt(K) / s[:KA]).astype(np.float32),
        "w4_words": w4_words, "w4_scales": w4_scales,
        "stain": (1.0 + 0.6 * n((H, S))).astype(np.float32),
        "gain": (np.exp(0.3 * n(H)) * u[:, 0]).astype(np.float32),
        "shift": (n(H) * u[:, 0]).astype(np.float32),
        "wa": wa.astype(np.float32),
        "w8_words": w8_words, "w8_scales": w8_scales,
        "res": n((N, P)).astype(np.float32),
    }

def reference(tab_words, tab_scales, offs, pos1, pos2, w1, w4_words, w4_scales,
              stain, gain, shift, wa, w8_words, w8_scales, res):
    v = unpack_weight(tab_words, tab_scales, "e4m3")[:, unstriped(offs)]
    w4 = unpack_weight(w4_words, w4_scales, "e2m1")
    w8 = unpack_weight(w8_words, w8_scales, "e4m3")
    raw = mxq(f64(w1), 0, "e4m3").T @ v[:KA] + w4.T @ v[KA:]
    h = f64(gain)[:, None] * (f64(stain) * raw)
    xa = np.abs(h[:, unstriped(pos1)])
    xb = h[:, unstriped(pos2)] + f64(shift)[:, None]
    ya = mxq(f64(wa), 0, "e4m3").T @ mxq(xa, 0, "e4m3")
    yb = w8.T @ mxq(xb, 0, "e4m3")
    y = (yb + f64(res)) * ya
    words, scales = planes(y)
    return y, words, scales

@@ -1,0 +1,293 @@
+from contextlib import ExitStack
+
+import concourse.mybir as mybir
+
+F32 = mybir.dt.float32
+BF16 = mybir.dt.bfloat16
+I32 = mybir.dt.int32
+U32 = mybir.dt.uint32
+U16 = mybir.dt.uint16
+U8 = mybir.dt.uint8
+FP8X4 = mybir.dt.float8_e4m3fn_x4
+FP4X4 = mybir.dt.float4_e2m1fn_x4
+MULT = mybir.AluOpType.mult
+ADD = mybir.AluOpType.add
+ACT = mybir.ActivationFunctionType
+
+P = 128
+T = 2048
+S = 1024
+H = 1024
+N = 512
+J = 512
+BANK = 512
+JH = 256
+
+FLOPS = 2 * 1536 * H * S + 2 * 2 * H * N * J
+
+
+def tile_list_karyotype_arm_features_kernel(
+    tc, tab_words, tab_scales, offs, pos1, pos2, w1, w4_words, w4_scales,
+    stain, gain, shift, wa, w8_words, w8_scales, res, out_0, out_1, out_2,
+):
+    nc = tc.nc
+    with ExitStack() as ctx:
+        lists = ctx.enter_context(tc.tile_pool(name="lists", bufs=1))
+        sb = ctx.enter_context(tc.tile_pool(name="sb", bufs=1))
+        psum = ctx.enter_context(tc.psum_pool(name="psum", bufs=8))
+
+        def tile(shape, dtype, name, tag=None, bufs=1):
+            return sb.tile(shape, dtype, name=name, tag=tag or name, bufs=bufs, align_bytes=64)
+
+        def zeroed_plane(width, name):
+            plane = tile([P, width], U8, name)
+            nc.vector.memset(plane[:].bitcast(I32), 0)
+            return plane
+
+        offs_t = lists.tile([P, S // 16], U16, name="offs_t")
+        pos1_t = lists.tile([P, J // 16], U16, name="pos1_t")
+        pos2_t = lists.tile([P, J // 16], U16, name="pos2_t")
+
+        tabs = zeroed_plane(T, "tabs")
+        w4s_raw = zeroed_plane(2 * H, "w4s_raw")
+        gs2 = zeroed_plane(S, "gs2")
+        w8s_raw = zeroed_plane(N, "w8s_raw")
+
+        tabw = [tile([P, T], U32, "tabw%d" % a) for a in range(3)]
+        w1_raw = [tile([P, 4, 512], F32, "w1_raw%d" % b, tag="wraw%d" % b) for b in range(2)]
+        w4_raw = [tile([P, 2, 1024], U8, "w4_raw%d" % b) for b in range(2)]
+        stain_t = [tile([P, S], F32, "stain%d" % s) for s in range(8)]
+        gain_t = tile([P, 2, 4], F32, "gain_t")
+        shift_t = tile([P, 2, 4], F32, "shift_t")
+        w8_raw = tile([P, 2, N], I32, "w8_raw")
+        res_t = tile([P, 4, J], F32, "res_t")
+        stain_rows = stain.rearrange("(b p t) m -> b t p m", b=2, t=4)
+
+        def load_tab(a):
+            nc.sync.dma_start(out=tabw[a][:].bitcast(I32),
+                              in_=tab_words[a].rearrange("p n i -> p (n i)").bitcast(I32))
+
+        def load_w1(b):
+            nc.sync.dma_start(out=w1_raw[b][:],
+                              in_=w1[:, 512 * b:512 * (b + 1)].rearrange("(p j) c -> p j c", j=4))
+
+        def load_w4(b):
+            nc.sync.dma_start(out=w4_raw[b][:].bitcast(I32),
+                              in_=w4_words[:, :, 1024 * b:1024 * (b + 1)].rearrange("a p c -> p a c").bitcast(I32))
+
+        def load_stain(s):
+            nc.sync.dma_start(out=stain_t[s][:], in_=stain_rows[s // 4, s % 4])
+
+        nc.sync.dma_start(offs_t[:], offs)
+        load_tab(0)
+        for q in range(4):
+            nc.sync.dma_start(out=tabs[32 * q:32 * q + 8, :].bitcast(I32),
+                              in_=tab_scales[1:3, 4 * q:4 * q + 4, :].bitcast(I32))
+        for q in range(4):
+            nc.sync.dma_start(out=tabs[32 * q + 8:32 * q + 12, :].bitcast(I32),
+                              in_=tab_scales[0, 4 * q:4 * q + 4, :].bitcast(I32))
+        load_tab(1)
+        load_w1(0)
+        for q in range(4):
+            nc.sync.dma_start(
+                out=w4s_raw[32 * q:32 * q + 4, :].bitcast(I32).rearrange("r (a c) -> r a c", a=2),
+                in_=w4_scales[:, 4 * q:4 * q + 4, :].bitcast(I32).rearrange("a r c -> r a c"))
+        load_w4(0)
+        load_tab(2)
+        nc.sync.dma_start(out=gain_t[:], in_=gain.rearrange("(b p t) -> p b t", b=2, t=4))
+        load_stain(0)
+        load_w1(1)
+        load_stain(1)
+        nc.sync.dma_start(pos2_t[:], pos2)
+        nc.sync.dma_start(pos1_t[:], pos1)
+        nc.sync.dma_start(out=shift_t[:], in_=shift.rearrange("(b p t) -> p b t", b=2, t=4))
+        load_w4(1)
+        for s in (2, 3, 5, 4, 6):
+            load_stain(s)
+
+        gw = [tile([P, S], U32, "gw%d" % a) for a in range(3)]
+        gs = tile([P, S], U8, "gs")
+        nc.vector.tensor_copy(gw[0][:], tabw[0][:].indirect(offs_t[:]))
+        nc.vector.tensor_copy(gs[:], tabs[:].indirect(offs_t[:]))
+        for q in range(4):
+            nc.scalar.dma_start(out=gs2[32 * q:32 * q + 4, :].bitcast(I32),
+                                in_=gs[32 * q + 4:32 * q + 8, :].bitcast(I32))
+        nc.vector.tensor_copy(gw[1][:], tabw[1][:].indirect(offs_t[:]))
+
+        def round_weight(raw, name):
+            rounded = tile([P, 2048], BF16, name, tag="rounded", bufs=6)
+            nc.scalar.copy(out=rounded[:].rearrange("p (t m j) -> p m j t", t=4, j=4),
+                           in_=raw[:].rearrange("p j (m t) -> p m j t", t=4))
+            return rounded
+
+        def quantize(rounded, name):
+            codes = tile([P, 512], U32, name + "_codes")
+            plane = tile([P, 512], U8, name + "_plane")
+            nc.vector.quantize_mx(out=codes[:].bitcast(FP8X4), scales=plane[:], in_=rounded[:])
+            return codes, plane
+
+        def deal_w4(b):
+            words = tile([P, 2, 1024], U8, "w4_dealt%d" % b)
+            nc.vector.tensor_copy(
+                out=words[:].bitcast(U16).rearrange("p a (t m) -> p a t m", t=4),
+                in_=w4_raw[b][:].bitcast(U16).rearrange("p a (m t) -> p a t m", t=4))
+            return words
+
+        w4s_dealt = tile([P, 4, 512], U8, "w4s_dealt")
+        nc.vector.tensor_copy(
+            out=w4s_dealt[:].rearrange("p g (t m) -> p g t m", t=4),
+            in_=w4s_raw[:].rearrange("p (g m t) -> p g t m", g=4, t=4))
+        w4_dealt = [deal_w4(0)]
+        w1q = [quantize(round_weight(w1_raw[0], "w1_rounded0"), "w1q0")]
+        nc.vector.tensor_copy(gw[2][:, 0:512], tabw[2][:].indirect(offs_t[:, 0:32]))
+        nc.vector.tensor_copy(gw[2][:, 512:1024], tabw[2][:].indirect(offs_t[:, 32:64]))
+        w4_dealt.append(deal_w4(1))
+
+        moving_planes = [gs[8:P, :], gs[:], gs2[:]]
+
+        def make_h(s):
+            b, t = divmod(s, 4)
+            h = tile([P, S], F32, "h%d" % s)
+            cols = slice(128 * t, 128 * (t + 1))
+            for half in range(2):
+                m = slice(BANK * half, BANK * (half + 1))
+                bank = psum.tile([P, BANK], F32, name="raw_bank", tag="bank")
+                for a in (1, 2):
+                    nc.tensor.matmul_mx(
+                        out=bank[:],
+                        lhsT=w4_dealt[b][:, a - 1, 256 * t:256 * (t + 1)].bitcast(FP4X4),
+                        lhsT_scale=w4s_dealt[:, 2 * (a - 1) + b, cols],
+                        rhs=gw[a][:, m].bitcast(FP8X4), rhs_scale=moving_planes[a][:, m],
+                        start=(a == 1), stop=False)
+                nc.tensor.matmul_mx(
+                    out=bank[:], lhsT=w1q[b][0][:, cols].bitcast(FP8X4), lhsT_scale=w1q[b][1][:, cols],
+                    rhs=gw[0][:, m].bitcast(FP8X4), rhs_scale=moving_planes[0][:, m],
+                    start=False, stop=True)
+                if t == 0:
+                    nc.vector.scalar_tensor_tensor(
+                        out=h[:, m], in0=bank[:], scalar=gain_t[:, b, t:t + 1], in1=stain_t[s][:, m],
+                        op0=MULT, op1=MULT)
+                else:
+                    nc.scalar.activation(out=h[:, m], in_=bank[:], func=ACT.Copy, scale=gain_t[:, b, t:t + 1])
+                    nc.gpsimd.tensor_tensor(out=h[:, m], in0=h[:, m], in1=stain_t[s][:, m], op=MULT)
+            return h
+
+        def short_arm(h, b, t, rows, tag, bufs):
+            picked = tile([P, J], F32, "picked2_%d" % (4 * b + t), tag=tag, bufs=bufs)
+            nc.vector.tensor_copy(picked[:], h[:].indirect(pos2_t[:]))
+            nc.scalar.activation(out=rows[:, t, :], in_=picked[:], func=ACT.Identity,
+                                 bias=shift_t[:, b, t:t + 1])
+
+        def weave_out(dst):
+            return dst.rearrange("p (c i t) -> p c t i", i=4, t=4)
+
+        def weave_in(src):
+            return src.rearrange("p t (c i) -> p c t i", i=4)
+
+        xb_rows = tile([P, 4, J], BF16, "xb_rows0", tag="rounded", bufs=6)
+        long0 = tile([P, 4, J], F32, "long0", tag="long0")
+        hs = {0: make_h(0)}
+        w1q.append(quantize(round_weight(w1_raw[1], "w1_rounded1"), "w1q1"))
+        for s in (1, 2, 3, 5, 6, 4):
+            hs[s] = make_h(s)
+
+        wa_raw = [tile([P, 4, 512], F32, "wa_raw%d" % b, tag="wraw%d" % b) for b in range(2)]
+
+        def load_wa(b):
+            nc.sync.dma_start(out=wa_raw[b][:],
+                              in_=wa[512 * b:512 * (b + 1), :].rearrange("(p j) c -> p j c", j=4))
+
+        load_stain(7)
+        hs[7] = make_h(7)
+        load_wa(0)
+        nc.sync.dma_start(out=w8_raw[:], in_=w8_words.rearrange("a p c i -> p a (c i)").bitcast(I32))
+        for q in range(4):
+            nc.sync.dma_start(out=w8s_raw[32 * q:32 * q + 8, :].bitcast(I32),
+                              in_=w8_scales[:, 4 * q:4 * q + 4, :].bitcast(I32))
+        load_wa(1)
+        nc.sync.dma_start(out=res_t[:], in_=res.rearrange("(p t) j -> p t j", t=4))
+
+        for t in range(4):
+            short_arm(hs[t], 0, t, xb_rows, "picked2", 4)
+            nc.vector.tensor_copy(long0[:, t, :], hs[t][:].indirect(pos1_t[:]))
+        xb_woven = tile([P, 2048], BF16, "xb_woven0", tag="rounded", bufs=6)
+        nc.scalar.copy(out=weave_out(xb_woven[:]), in_=weave_in(xb_rows[:]))
+        xa_woven = tile([P, 2048], BF16, "xa_woven0", tag="rounded", bufs=6)
+        nc.scalar.activation(out=weave_out(xa_woven[:]), in_=weave_in(long0[:]), func=ACT.Abs)
+
+        xb_rows = tile([P, 4, J], BF16, "xb_rows1", tag="rounded", bufs=6)
+        for t in range(4):
+            short_arm(hs[4 + t], 1, t, xb_rows, "picked2", 4)
+        xbq = [quantize(xb_woven, "xbq0")]
+        xaq = [quantize(xa_woven, "xaq0")]
+        xb_woven = tile([P, 2048], BF16, "xb_woven1", tag="rounded", bufs=6)
+        nc.scalar.copy(out=weave_out(xb_woven[:]), in_=weave_in(xb_rows[:]))
+        w8_dealt = tile([P, 2, N], I32, "w8_dealt")
+        w8s_dealt = tile([P, N], U8, "w8s_dealt")
+        nc.vector.tensor_copy(out=w8_dealt[:].rearrange("p a (t m) -> p a m t", t=4),
+                              in_=w8_raw[:].rearrange("p a (m t) -> p a m t", t=4))
+        nc.vector.tensor_copy(out=w8s_dealt[:].rearrange("p (t m) -> p t m", t=4),
+                              in_=w8s_raw[:].rearrange("p (m t) -> p t m", t=4))
+        xbq.append(quantize(xb_woven, "xbq1"))
+        waq = [quantize(round_weight(wa_raw[b], "wa_rounded%d" % b), "waq%d" % b) for b in range(2)]
+        long1 = tile([P, 2, 4, JH], F32, "long1", tag="stain7")
+        for jh in range(2):
+            for t in range(4):
+                nc.vector.tensor_copy(long1[:, jh, t, :], hs[4 + t][:].indirect(pos1_t[:, 16 * jh:16 * (jh + 1)]))
+        xa_codes = tile([P, 512], U32, "xaq1_codes")
+        xa_plane = tile([P, 512], U8, "xaq1_plane")
+        xaq.append((xa_codes, xa_plane))
+
+        def second_stage(stationary, moving, jh, tp):
+            bank = psum.tile([P, 2, JH], F32, name="y_bank", tag="bank")
+            cols = slice(JH * jh, JH * (jh + 1))
+            for b in range(2):
+                for u in range(2):
+                    codes, plane = stationary(b, slice(128 * (2 * tp + u), 128 * (2 * tp + u + 1)))
+                    nc.tensor.matmul_mx(
+                        out=bank[:, u, :], lhsT=codes.bitcast(FP8X4), lhsT_scale=plane,
+                        rhs=moving[b][0][:, cols].bitcast(FP8X4), rhs_scale=moving[b][1][:, cols],
+                        start=(b == 0 and u == 0), stop=(b == 1 and u == 1))
+            return bank
+
+        def w8_cols(b, n):
+            return w8_dealt[:, b, n], w8s_dealt[4 * b:P, n]
+
+        def wa_cols(b, n):
+            return waq[b][0][:, n], waq[b][1][:, n]
+
+        shifted = tile([P, 2, 4, JH], F32, "shifted", tag="long0")
+        for jh in range(2):
+            for tp in range(2):
+                bank = second_stage(w8_cols, xbq, jh, tp)
+                nc.vector.tensor_tensor(out=shifted[:, jh, 2 * tp:2 * tp + 2, :], in0=bank[:],
+                                        in1=res_t[:, 2 * tp:2 * tp + 2, JH * jh:JH * (jh + 1)], op=ADD)
+
+        y_codes = tile([P, J], U32, "y_codes")
+        y_plane = tile([P, J], U8, "y_plane")
+        out_rows = out_0.rearrange("(p t) j -> p t j", t=4)
+        out_words = out_1[0].rearrange("p m i -> p (m i)").bitcast(I32)
+        for jh in range(2):
+            cols = slice(JH * jh, JH * (jh + 1))
+            xa_woven = tile([P, 4 * JH], BF16, "xa_woven1_%d" % jh)
+            nc.scalar.activation(out=weave_out(xa_woven[:]), in_=weave_in(long1[:, jh]), func=ACT.Abs)
+            nc.vector.quantize_mx(out=xa_codes[:, cols].bitcast(FP8X4), scales=xa_plane[:, cols], in_=xa_woven[:])
+        for jh in range(2):
+            cols = slice(JH * jh, JH * (jh + 1))
+            y = tile([P, 4, JH], F32, "y%d" % jh)
+            for tp in range(2):
+                bank = second_stage(wa_cols, xaq, jh, tp)
+                nc.vector.tensor_tensor(out=y[:, 2 * tp:2 * tp + 2, :], in0=bank[:],
+                                        in1=shifted[:, jh, 2 * tp:2 * tp + 2, :], op=MULT)
+            nc.sync.dma_start(out=out_rows[:, :, cols], in_=y[:])
+            y_woven = tile([P, 4 * JH], BF16, "y_woven%d" % jh)
+            if jh == 0:
+                nc.scalar.copy(out=weave_out(y_woven[:]), in_=weave_in(y[:]))
+            else:
+                nc.vector.tensor_copy(out=weave_out(y_woven[:]), in_=weave_in(y[:]))
+            nc.vector.quantize_mx(out=y_codes[:, cols].bitcast(FP8X4), scales=y_plane[:, cols], in_=y_woven[:])
+            nc.sync.dma_start(out=out_words[:, cols], in_=y_codes[:, cols].bitcast(I32))
+        for q in range(4):
+            queue = nc.sync if q % 2 == 0 else nc.scalar
+            queue.dma_start(out=out_2[0, 4 * q:4 * q + 4, :].bitcast(I32),
+                            in_=y_plane[32 * q:32 * q + 4, :].bitcast(I32))

@@ -34,6 +34,7 @@ def tile_list_karyotype_arm_features_kernel(
     with ExitStack() as ctx:
         lists = ctx.enter_context(tc.tile_pool(name="lists", bufs=1))
         sb = ctx.enter_context(tc.tile_pool(name="sb", bufs=1))
+        late = ctx.enter_context(tc.tile_pool(name="late", bufs=1))
         psum = ctx.enter_context(tc.psum_pool(name="psum", bufs=8))
 
         def tile(shape, dtype, name, tag=None, bufs=1):
@@ -54,10 +55,13 @@ def tile_list_karyotype_arm_features_kernel(
         w8s_raw = zeroed_plane(N, "w8s_raw")
 
         tabw = [tile([P, T], U32, "tabw%d" % a) for a in range(3)]
-        w1_raw = [tile([P, 4, 512], F32, "w1_raw%d" % b, tag="wraw%d" % b) for b in range(2)]
+        w1_raw = [tile([P, 4, 512], F32, "w1_raw%d" % b) for b in range(2)]
+        wa_raw = [tile([P, 4, 512], F32, "wa_raw%d" % b) for b in range(2)]
         w4_raw = [tile([P, 2, 1024], U8, "w4_raw%d" % b) for b in range(2)]
-        stain_t = [tile([P, S], F32, "stain%d" % s) for s in range(8)]
+        stain_t = [tile([P, S], F32, "stain%d" % s) for s in range(7)]
+        stain_t.append(late.tile([P, S], F32, name="stain7", offset=3072, align_bytes=64))
         gain_t = tile([P, 2, 4], F32, "gain_t")
+        gain_s = tile([P, 2, 4], F32, "gain_s", tag="xb_rows0")
         shift_t = tile([P, 2, 4], F32, "shift_t")
         w8_raw = tile([P, 2, N], I32, "w8_raw")
         res_t = tile([P, 4, J], F32, "res_t")
@@ -71,6 +75,10 @@ def tile_list_karyotype_arm_features_kernel(
             nc.sync.dma_start(out=w1_raw[b][:],
                               in_=w1[:, 512 * b:512 * (b + 1)].rearrange("(p j) c -> p j c", j=4))
 
+        def load_wa(b):
+            nc.sync.dma_start(out=wa_raw[b][:],
+                              in_=wa[512 * b:512 * (b + 1), :].rearrange("(p j) c -> p j c", j=4))
+
         def load_w4(b):
             nc.sync.dma_start(out=w4_raw[b][:].bitcast(I32),
                               in_=w4_words[:, :, 1024 * b:1024 * (b + 1)].rearrange("a p c -> p a c").bitcast(I32))
@@ -78,41 +86,59 @@ def tile_list_karyotype_arm_features_kernel(
         def load_stain(s):
             nc.sync.dma_start(out=stain_t[s][:], in_=stain_rows[s // 4, s % 4])
 
+        def load_tab_scales(passes, row):
+            for q in range(4):
+                rows = slice(32 * q + row, 32 * q + row + 4 * len(passes))
+                nc.sync.dma_start(out=tabs[rows, :].bitcast(I32),
+                                  in_=tab_scales[passes.start:passes.stop, 4 * q:4 * q + 4, :].bitcast(I32))
+
         nc.sync.dma_start(offs_t[:], offs)
         load_tab(0)
-        for q in range(4):
-            nc.sync.dma_start(out=tabs[32 * q:32 * q + 8, :].bitcast(I32),
-                              in_=tab_scales[1:3, 4 * q:4 * q + 4, :].bitcast(I32))
-        for q in range(4):
-            nc.sync.dma_start(out=tabs[32 * q + 8:32 * q + 12, :].bitcast(I32),
-                              in_=tab_scales[0, 4 * q:4 * q + 4, :].bitcast(I32))
+        load_tab_scales(range(1, 3), 0)
         load_tab(1)
+        load_tab_scales(range(0, 1), 8)
         load_w1(0)
         for q in range(4):
             nc.sync.dma_start(
                 out=w4s_raw[32 * q:32 * q + 4, :].bitcast(I32).rearrange("r (a c) -> r a c", a=2),
                 in_=w4_scales[:, 4 * q:4 * q + 4, :].bitcast(I32).rearrange("a r c -> r a c"))
         load_w4(0)
-        load_tab(2)
-        nc.sync.dma_start(out=gain_t[:], in_=gain.rearrange("(b p t) -> p b t", b=2, t=4))
-        load_stain(0)
-        load_w1(1)
-        load_stain(1)
-        nc.sync.dma_start(pos2_t[:], pos2)
-        nc.sync.dma_start(pos1_t[:], pos1)
-        nc.sync.dma_start(out=shift_t[:], in_=shift.rearrange("(b p t) -> p b t", b=2, t=4))
         load_w4(1)
-        for s in (2, 3, 5, 4, 6):
-            load_stain(s)
+        load_w1(1)
+        load_tab(2)
 
         gw = [tile([P, S], U32, "gw%d" % a) for a in range(3)]
         gs = tile([P, S], U8, "gs")
         nc.vector.tensor_copy(gw[0][:], tabw[0][:].indirect(offs_t[:]))
         nc.vector.tensor_copy(gs[:], tabs[:].indirect(offs_t[:]))
-        for q in range(4):
-            nc.scalar.dma_start(out=gs2[32 * q:32 * q + 4, :].bitcast(I32),
-                                in_=gs[32 * q + 4:32 * q + 8, :].bitcast(I32))
         nc.vector.tensor_copy(gw[1][:], tabw[1][:].indirect(offs_t[:]))
+        for q in range(4):
+            nc.sync.dma_start(out=gs2[32 * q:32 * q + 4, :].bitcast(I32),
+                              in_=gs[32 * q + 4:32 * q + 8, :].bitcast(I32))
+
+        load_wa(0)
+        load_stain(0)
+        nc.sync.dma_start(out=gain_t[:], in_=gain.rearrange("(b p t) -> p b t", b=2, t=4))
+        nc.sync.dma_start(out=gain_s[:], in_=gain.rearrange("(b p t) -> p b t", b=2, t=4))
+        load_stain(1)
+        nc.sync.dma_start(pos2_t[:], pos2)
+        nc.sync.dma_start(pos1_t[:], pos1)
+        nc.sync.dma_start(out=shift_t[:], in_=shift.rearrange("(b p t) -> p b t", b=2, t=4))
+        for x in (2, "wa1", 3, 5, 6, 7, 4, "w8"):
+            if x == "w1":
+                load_w1(1)
+            elif x == "wa0":
+                load_wa(0)
+            elif x == "wa1":
+                load_wa(1)
+            elif x == "w8":
+                nc.sync.dma_start(out=w8_raw[:], in_=w8_words.rearrange("a p c i -> p a (c i)").bitcast(I32))
+                for q in range(4):
+                    nc.sync.dma_start(out=w8s_raw[32 * q:32 * q + 8, :].bitcast(I32),
+                                      in_=w8_scales[:, 4 * q:4 * q + 4, :].bitcast(I32))
+            else:
+                load_stain(x)
+        nc.sync.dma_start(out=res_t[:], in_=res.rearrange("(p t) j -> p t j", t=4))
 
         def round_weight(raw, name):
             rounded = tile([P, 2048], BF16, name, tag="rounded", bufs=6)
@@ -120,9 +146,12 @@ def tile_list_karyotype_arm_features_kernel(
                            in_=raw[:].rearrange("p j (m t) -> p m j t", t=4))
             return rounded
 
-        def quantize(rounded, name):
+        def quantize(rounded, name, place=None):
             codes = tile([P, 512], U32, name + "_codes")
-            plane = tile([P, 512], U8, name + "_plane")
+            if place is None:
+                plane = tile([P, 512], U8, name + "_plane")
+            else:
+                plane = late.tile([P, 512], U8, name=name + "_plane", offset=4096 + 512 * place, align_bytes=64)
             nc.vector.quantize_mx(out=codes[:].bitcast(FP8X4), scales=plane[:], in_=rounded[:])
             return codes, plane
 
@@ -134,14 +163,14 @@ def tile_list_karyotype_arm_features_kernel(
             return words
 
         w4s_dealt = tile([P, 4, 512], U8, "w4s_dealt")
-        nc.vector.tensor_copy(
-            out=w4s_dealt[:].rearrange("p g (t m) -> p g t m", t=4),
-            in_=w4s_raw[:].rearrange("p (g m t) -> p g t m", g=4, t=4))
-        w4_dealt = [deal_w4(0)]
-        w1q = [quantize(round_weight(w1_raw[0], "w1_rounded0"), "w1q0")]
+        for g in (0, 2, 1, 3):
+            nc.vector.tensor_copy(
+                out=w4s_dealt[:, g, :].rearrange("p (t m) -> p t m", t=4),
+                in_=w4s_raw[:, 512 * g:512 * (g + 1)].rearrange("p (m t) -> p t m", t=4))
+        w4_dealt = [deal_w4(0), deal_w4(1)]
+        w1q = [quantize(round_weight(w1_raw[b], "w1_rounded%d" % b), "w1q%d" % b) for b in range(2)]
         nc.vector.tensor_copy(gw[2][:, 0:512], tabw[2][:].indirect(offs_t[:, 0:32]))
         nc.vector.tensor_copy(gw[2][:, 512:1024], tabw[2][:].indirect(offs_t[:, 32:64]))
-        w4_dealt.append(deal_w4(1))
 
         moving_planes = [gs[8:P, :], gs[:], gs2[:]]
 
@@ -149,27 +178,29 @@ def tile_list_karyotype_arm_features_kernel(
             b, t = divmod(s, 4)
             h = tile([P, S], F32, "h%d" % s)
             cols = slice(128 * t, 128 * (t + 1))
+            order = (0, 1, 2) if s == 0 else (2, 0, 1)
             for half in range(2):
                 m = slice(BANK * half, BANK * (half + 1))
                 bank = psum.tile([P, BANK], F32, name="raw_bank", tag="bank")
-                for a in (1, 2):
+                for a in order:
+                    if a == 0:
+                        codes, plane = w1q[b][0][:, cols].bitcast(FP8X4), w1q[b][1][:, cols]
+                    else:
+                        codes = w4_dealt[b][:, a - 1, 256 * t:256 * (t + 1)].bitcast(FP4X4)
+                        plane = w4s_dealt[:, 2 * (a - 1) + b, cols]
                     nc.tensor.matmul_mx(
-                        out=bank[:],
-                        lhsT=w4_dealt[b][:, a - 1, 256 * t:256 * (t + 1)].bitcast(FP4X4),
-                        lhsT_scale=w4s_dealt[:, 2 * (a - 1) + b, cols],
+                        out=bank[:], lhsT=codes, lhsT_scale=plane,
                         rhs=gw[a][:, m].bitcast(FP8X4), rhs_scale=moving_planes[a][:, m],
-                        start=(a == 1), stop=False)
-                nc.tensor.matmul_mx(
-                    out=bank[:], lhsT=w1q[b][0][:, cols].bitcast(FP8X4), lhsT_scale=w1q[b][1][:, cols],
-                    rhs=gw[0][:, m].bitcast(FP8X4), rhs_scale=moving_planes[0][:, m],
-                    start=False, stop=True)
-                if t == 0:
+                        start=(a == order[0]), stop=(a == order[-1]))
+                if s in (0, 4):
                     nc.vector.scalar_tensor_tensor(
                         out=h[:, m], in0=bank[:], scalar=gain_t[:, b, t:t + 1], in1=stain_t[s][:, m],
                         op0=MULT, op1=MULT)
                 else:
-                    nc.scalar.activation(out=h[:, m], in_=bank[:], func=ACT.Copy, scale=gain_t[:, b, t:t + 1])
-                    nc.gpsimd.tensor_tensor(out=h[:, m], in0=h[:, m], in1=stain_t[s][:, m], op=MULT)
+                    nc.scalar.activation(out=h[:, m], in_=bank[:], func=ACT.Copy, scale=gain_s[:, b, t:t + 1])
+                    for c0 in range(m.start, m.stop, 512):
+                        c = slice(c0, c0 + 512)
+                        nc.gpsimd.tensor_tensor(out=h[:, c], in0=h[:, c], in1=stain_t[s][:, c], op=MULT)
             return h
 
         def short_arm(h, b, t, rows, tag, bufs):
@@ -184,29 +215,13 @@ def tile_list_karyotype_arm_features_kernel(
         def weave_in(src):
             return src.rearrange("p t (c i) -> p c t i", i=4)
 
-        xb_rows = tile([P, 4, J], BF16, "xb_rows0", tag="rounded", bufs=6)
-        long0 = tile([P, 4, J], F32, "long0", tag="long0")
-        hs = {0: make_h(0)}
-        w1q.append(quantize(round_weight(w1_raw[1], "w1_rounded1"), "w1q1"))
-        for s in (1, 2, 3, 5, 6, 4):
+        xb_rows = tile([P, 4, J], BF16, "xb_rows0")
+        long0 = tile([P, 4, J], F32, "long0", tag="w1_raw0")
+        hs = {s: make_h(s) for s in (0, 1, 2)}
+        for s in (3, 5, 6, 7, 4):
             hs[s] = make_h(s)
 
-        wa_raw = [tile([P, 4, 512], F32, "wa_raw%d" % b, tag="wraw%d" % b) for b in range(2)]
-
-        def load_wa(b):
-            nc.sync.dma_start(out=wa_raw[b][:],
-                              in_=wa[512 * b:512 * (b + 1), :].rearrange("(p j) c -> p j c", j=4))
-
-        load_stain(7)
-        hs[7] = make_h(7)
-        load_wa(0)
-        nc.sync.dma_start(out=w8_raw[:], in_=w8_words.rearrange("a p c i -> p a (c i)").bitcast(I32))
-        for q in range(4):
-            nc.sync.dma_start(out=w8s_raw[32 * q:32 * q + 8, :].bitcast(I32),
-                              in_=w8_scales[:, 4 * q:4 * q + 4, :].bitcast(I32))
-        load_wa(1)
-        nc.sync.dma_start(out=res_t[:], in_=res.rearrange("(p t) j -> p t j", t=4))
-
+        wa_rounded = [round_weight(wa_raw[b], "wa_rounded%d" % b) for b in range(2)]
         for t in range(4):
             short_arm(hs[t], 0, t, xb_rows, "picked2", 4)
             nc.vector.tensor_copy(long0[:, t, :], hs[t][:].indirect(pos1_t[:]))
@@ -218,22 +233,25 @@ def tile_list_karyotype_arm_features_kernel(
         xb_rows = tile([P, 4, J], BF16, "xb_rows1", tag="rounded", bufs=6)
         for t in range(4):
             short_arm(hs[4 + t], 1, t, xb_rows, "picked2", 4)
-        xbq = [quantize(xb_woven, "xbq0")]
-        xaq = [quantize(xa_woven, "xaq0")]
-        xb_woven = tile([P, 2048], BF16, "xb_woven1", tag="rounded", bufs=6)
-        nc.scalar.copy(out=weave_out(xb_woven[:]), in_=weave_in(xb_rows[:]))
+        xb_woven1 = tile([P, 2048], BF16, "xb_woven1", tag="rounded", bufs=6)
+        nc.scalar.copy(out=weave_out(xb_woven1[:]), in_=weave_in(xb_rows[:]))
         w8_dealt = tile([P, 2, N], I32, "w8_dealt")
         w8s_dealt = tile([P, N], U8, "w8s_dealt")
-        nc.vector.tensor_copy(out=w8_dealt[:].rearrange("p a (t m) -> p a m t", t=4),
+        nc.gpsimd.tensor_copy(out=w8_dealt[:].rearrange("p a (t m) -> p a m t", t=4),
                               in_=w8_raw[:].rearrange("p a (m t) -> p a m t", t=4))
-        nc.vector.tensor_copy(out=w8s_dealt[:].rearrange("p (t m) -> p t m", t=4),
+        nc.gpsimd.tensor_copy(out=w8s_dealt[:].rearrange("p (t m) -> p t m", t=4),
                               in_=w8s_raw[:].rearrange("p (m t) -> p t m", t=4))
-        xbq.append(quantize(xb_woven, "xbq1"))
-        waq = [quantize(round_weight(wa_raw[b], "wa_rounded%d" % b), "waq%d" % b) for b in range(2)]
-        long1 = tile([P, 2, 4, JH], F32, "long1", tag="stain7")
-        for jh in range(2):
+        long1 = [late.tile([P, 4, JH], F32, name="long1_%d" % jh, offset=6144 * jh, align_bytes=64) for jh in range(2)]
+
+        def pick_long(jh):
             for t in range(4):
-                nc.vector.tensor_copy(long1[:, jh, t, :], hs[4 + t][:].indirect(pos1_t[:, 16 * jh:16 * (jh + 1)]))
+                nc.vector.tensor_copy(long1[jh][:, t, :], hs[4 + t][:].indirect(pos1_t[:, 16 * jh:16 * (jh + 1)]))
+
+        pick_long(0)
+        xbq = [quantize(xb_woven, "xbq0", 0), quantize(xb_woven1, "xbq1")]
+        xaq = [quantize(xa_woven, "xaq0", 1)]
+        waq = [quantize(wa_rounded[b], "waq%d" % b, 2 + b) for b in range(2)]
+        pick_long(1)
         xa_codes = tile([P, 512], U32, "xaq1_codes")
         xa_plane = tile([P, 512], U8, "xaq1_plane")
         xaq.append((xa_codes, xa_plane))
@@ -256,7 +274,7 @@ def tile_list_karyotype_arm_features_kernel(
         def wa_cols(b, n):
             return waq[b][0][:, n], waq[b][1][:, n]
 
-        shifted = tile([P, 2, 4, JH], F32, "shifted", tag="long0")
+        shifted = tile([P, 2, 4, JH], F32, "shifted", tag="w1_raw1")
         for jh in range(2):
             for tp in range(2):
                 bank = second_stage(w8_cols, xbq, jh, tp)
@@ -270,11 +288,11 @@ def tile_list_karyotype_arm_features_kernel(
         for jh in range(2):
             cols = slice(JH * jh, JH * (jh + 1))
             xa_woven = tile([P, 4 * JH], BF16, "xa_woven1_%d" % jh)
-            nc.scalar.activation(out=weave_out(xa_woven[:]), in_=weave_in(long1[:, jh]), func=ACT.Abs)
+            nc.scalar.activation(out=weave_out(xa_woven[:]), in_=weave_in(long1[jh][:]), func=ACT.Abs)
             nc.vector.quantize_mx(out=xa_codes[:, cols].bitcast(FP8X4), scales=xa_plane[:, cols], in_=xa_woven[:])
         for jh in range(2):
             cols = slice(JH * jh, JH * (jh + 1))
-            y = tile([P, 4, JH], F32, "y%d" % jh)
+            y = tile([P, 4, JH], F32, "y%d" % jh, tag="wa_raw%d" % jh)
             for tp in range(2):
                 bank = second_stage(wa_cols, xaq, jh, tp)
                 nc.vector.tensor_tensor(out=y[:, 2 * tp:2 * tp + 2, :], in0=bank[:],

@@ -57,9 +57,9 @@ def tile_list_karyotype_arm_features_kernel(
         tabw = [tile([P, T], U32, "tabw%d" % a) for a in range(3)]
         w1_raw = [tile([P, 4, 512], F32, "w1_raw%d" % b) for b in range(2)]
         wa_raw = [tile([P, 4, 512], F32, "wa_raw%d" % b) for b in range(2)]
-        w4_raw = [tile([P, 2, 1024], U8, "w4_raw%d" % b) for b in range(2)]
+        w4_raw = tile([P, 2, 2048], U8, "w4_raw")
         stain_t = [tile([P, S], F32, "stain%d" % s) for s in range(7)]
-        stain_t.append(late.tile([P, S], F32, name="stain7", offset=3072, align_bytes=64))
+        stain_t.append(late.tile([P, S], F32, name="stain7", offset=0, align_bytes=64))
         gain_t = tile([P, 2, 4], F32, "gain_t")
         gain_s = tile([P, 2, 4], F32, "gain_s", tag="xb_rows0")
         shift_t = tile([P, 2, 4], F32, "shift_t")
@@ -78,10 +78,6 @@ def tile_list_karyotype_arm_features_kernel(
         def load_wa(b):
             nc.sync.dma_start(out=wa_raw[b][:],
                               in_=wa[512 * b:512 * (b + 1), :].rearrange("(p j) c -> p j c", j=4))
-
-        def load_w4(b):
-            nc.sync.dma_start(out=w4_raw[b][:].bitcast(I32),
-                              in_=w4_words[:, :, 1024 * b:1024 * (b + 1)].rearrange("a p c -> p a c").bitcast(I32))
 
         def load_stain(s):
             nc.sync.dma_start(out=stain_t[s][:], in_=stain_rows[s // 4, s % 4])
@@ -102,8 +98,7 @@ def tile_list_karyotype_arm_features_kernel(
             nc.sync.dma_start(
                 out=w4s_raw[32 * q:32 * q + 4, :].bitcast(I32).rearrange("r (a c) -> r a c", a=2),
                 in_=w4_scales[:, 4 * q:4 * q + 4, :].bitcast(I32).rearrange("a r c -> r a c"))
-        load_w4(0)
-        load_w4(1)
+        nc.sync.dma_start(out=w4_raw[:].bitcast(I32), in_=w4_words.rearrange("a p c -> p a c").bitcast(I32))
         load_w1(1)
         load_tab(2)
 
@@ -117,20 +112,20 @@ def tile_list_karyotype_arm_features_kernel(
                               in_=gs[32 * q + 4:32 * q + 8, :].bitcast(I32))
 
         load_wa(0)
-        load_stain(0)
         nc.sync.dma_start(out=gain_t[:], in_=gain.rearrange("(b p t) -> p b t", b=2, t=4))
         nc.sync.dma_start(out=gain_s[:], in_=gain.rearrange("(b p t) -> p b t", b=2, t=4))
-        load_stain(1)
         nc.sync.dma_start(pos2_t[:], pos2)
+        load_stain(0)
         nc.sync.dma_start(pos1_t[:], pos1)
-        nc.sync.dma_start(out=shift_t[:], in_=shift.rearrange("(b p t) -> p b t", b=2, t=4))
-        for x in (2, "wa1", 3, 5, 6, 7, 4, "w8"):
+        for x in (1, 2, "shift", 3, 4, 5, "wa1", 6, 7, "w8"):
             if x == "w1":
                 load_w1(1)
             elif x == "wa0":
                 load_wa(0)
             elif x == "wa1":
                 load_wa(1)
+            elif x == "shift":
+                nc.sync.dma_start(out=shift_t[:], in_=shift.rearrange("(b p t) -> p b t", b=2, t=4))
             elif x == "w8":
                 nc.sync.dma_start(out=w8_raw[:], in_=w8_words.rearrange("a p c i -> p a (c i)").bitcast(I32))
                 for q in range(4):
@@ -141,7 +136,7 @@ def tile_list_karyotype_arm_features_kernel(
         nc.sync.dma_start(out=res_t[:], in_=res.rearrange("(p t) j -> p t j", t=4))
 
         def round_weight(raw, name):
-            rounded = tile([P, 2048], BF16, name, tag="rounded", bufs=6)
+            rounded = tile([P, 2048], BF16, name, tag="rounded", bufs=5)
             nc.scalar.copy(out=rounded[:].rearrange("p (t m j) -> p m j t", t=4, j=4),
                            in_=raw[:].rearrange("p j (m t) -> p m j t", t=4))
             return rounded
@@ -151,23 +146,17 @@ def tile_list_karyotype_arm_features_kernel(
             if place is None:
                 plane = tile([P, 512], U8, name + "_plane")
             else:
-                plane = late.tile([P, 512], U8, name=name + "_plane", offset=4096 + 512 * place, align_bytes=64)
+                plane = late.tile([P, 512], U8, name=name + "_plane", offset=512 * place, align_bytes=64)
             nc.vector.quantize_mx(out=codes[:].bitcast(FP8X4), scales=plane[:], in_=rounded[:])
             return codes, plane
 
-        def deal_w4(b):
-            words = tile([P, 2, 1024], U8, "w4_dealt%d" % b)
-            nc.vector.tensor_copy(
-                out=words[:].bitcast(U16).rearrange("p a (t m) -> p a t m", t=4),
-                in_=w4_raw[b][:].bitcast(U16).rearrange("p a (m t) -> p a t m", t=4))
-            return words
-
         w4s_dealt = tile([P, 4, 512], U8, "w4s_dealt")
-        for g in (0, 2, 1, 3):
-            nc.vector.tensor_copy(
-                out=w4s_dealt[:, g, :].rearrange("p (t m) -> p t m", t=4),
-                in_=w4s_raw[:, 512 * g:512 * (g + 1)].rearrange("p (m t) -> p t m", t=4))
-        w4_dealt = [deal_w4(0), deal_w4(1)]
+        nc.vector.tensor_copy(out=w4s_dealt[:].rearrange("p g (t m) -> p g t m", t=4),
+                              in_=w4s_raw[:].rearrange("p (g m t) -> p g t m", g=4, t=4))
+        w4_dealt = tile([P, 4, 1024], U8, "w4_dealt")
+        nc.vector.tensor_copy(
+            out=w4_dealt[:].bitcast(U16).rearrange("p g (t m) -> p g t m", t=4),
+            in_=w4_raw[:].bitcast(U16).rearrange("p a (b m t) -> p (a b) t m", b=2, t=4))
         w1q = [quantize(round_weight(w1_raw[b], "w1_rounded%d" % b), "w1q%d" % b) for b in range(2)]
         nc.vector.tensor_copy(gw[2][:, 0:512], tabw[2][:].indirect(offs_t[:, 0:32]))
         nc.vector.tensor_copy(gw[2][:, 512:1024], tabw[2][:].indirect(offs_t[:, 32:64]))
@@ -178,7 +167,7 @@ def tile_list_karyotype_arm_features_kernel(
             b, t = divmod(s, 4)
             h = tile([P, S], F32, "h%d" % s)
             cols = slice(128 * t, 128 * (t + 1))
-            order = (0, 1, 2) if s == 0 else (2, 0, 1)
+            order = (0, 1, 2) if s in (0, 2) else (2, 0, 1)
             for half in range(2):
                 m = slice(BANK * half, BANK * (half + 1))
                 bank = psum.tile([P, BANK], F32, name="raw_bank", tag="bank")
@@ -186,18 +175,18 @@ def tile_list_karyotype_arm_features_kernel(
                     if a == 0:
                         codes, plane = w1q[b][0][:, cols].bitcast(FP8X4), w1q[b][1][:, cols]
                     else:
-                        codes = w4_dealt[b][:, a - 1, 256 * t:256 * (t + 1)].bitcast(FP4X4)
+                        codes = w4_dealt[:, 2 * (a - 1) + b, 256 * t:256 * (t + 1)].bitcast(FP4X4)
                         plane = w4s_dealt[:, 2 * (a - 1) + b, cols]
                     nc.tensor.matmul_mx(
                         out=bank[:], lhsT=codes, lhsT_scale=plane,
                         rhs=gw[a][:, m].bitcast(FP8X4), rhs_scale=moving_planes[a][:, m],
                         start=(a == order[0]), stop=(a == order[-1]))
-                if s in (0, 4):
+                if (s, half) in ((0, 0), (0, 1), (1, 0), (1, 1), (4, 0), (4, 1)):
                     nc.vector.scalar_tensor_tensor(
                         out=h[:, m], in0=bank[:], scalar=gain_t[:, b, t:t + 1], in1=stain_t[s][:, m],
                         op0=MULT, op1=MULT)
                 else:
-                    nc.scalar.activation(out=h[:, m], in_=bank[:], func=ACT.Copy, scale=gain_s[:, b, t:t + 1])
+                    nc.scalar.activation(out=h[:, m], in_=bank[:], func=ACT.Copy, scale=(gain_s if s <= 5 else gain_t)[:, b, t:t + 1])
                     for c0 in range(m.start, m.stop, 512):
                         c = slice(c0, c0 + 512)
                         nc.gpsimd.tensor_tensor(out=h[:, c], in0=h[:, c], in1=stain_t[s][:, c], op=MULT)
@@ -217,37 +206,37 @@ def tile_list_karyotype_arm_features_kernel(
 
         xb_rows = tile([P, 4, J], BF16, "xb_rows0")
         long0 = tile([P, 4, J], F32, "long0", tag="w1_raw0")
-        hs = {s: make_h(s) for s in (0, 1, 2)}
-        for s in (3, 5, 6, 7, 4):
+        hs = {s: make_h(s) for s in (0, 2, 1)}
+        for s in (3, 5, 4, 6, 7):
             hs[s] = make_h(s)
 
         wa_rounded = [round_weight(wa_raw[b], "wa_rounded%d" % b) for b in range(2)]
         for t in range(4):
-            short_arm(hs[t], 0, t, xb_rows, "picked2", 4)
+            short_arm(hs[t], 0, t, xb_rows, "picked2", 6)
             nc.vector.tensor_copy(long0[:, t, :], hs[t][:].indirect(pos1_t[:]))
-        xb_woven = tile([P, 2048], BF16, "xb_woven0", tag="rounded", bufs=6)
+        xb_woven = tile([P, 2048], BF16, "xb_woven0", tag="rounded", bufs=5)
         nc.scalar.copy(out=weave_out(xb_woven[:]), in_=weave_in(xb_rows[:]))
-        xa_woven = tile([P, 2048], BF16, "xa_woven0", tag="rounded", bufs=6)
+        xa_woven = tile([P, 2048], BF16, "xa_woven0", tag="rounded", bufs=5)
         nc.scalar.activation(out=weave_out(xa_woven[:]), in_=weave_in(long0[:]), func=ACT.Abs)
 
-        xb_rows = tile([P, 4, J], BF16, "xb_rows1", tag="rounded", bufs=6)
+        xb_rows = tile([P, 4, J], BF16, "xb_rows1")
         for t in range(4):
-            short_arm(hs[4 + t], 1, t, xb_rows, "picked2", 4)
-        xb_woven1 = tile([P, 2048], BF16, "xb_woven1", tag="rounded", bufs=6)
+            short_arm(hs[4 + t], 1, t, xb_rows, "picked2", 6)
+        xb_woven1 = tile([P, 2048], BF16, "xb_woven1", tag="rounded", bufs=5)
         nc.scalar.copy(out=weave_out(xb_woven1[:]), in_=weave_in(xb_rows[:]))
         w8_dealt = tile([P, 2, N], I32, "w8_dealt")
-        w8s_dealt = tile([P, N], U8, "w8s_dealt")
+        w8s_dealt = late.tile([P, N], U8, name="w8s_dealt", offset=2048, align_bytes=64)
         nc.gpsimd.tensor_copy(out=w8_dealt[:].rearrange("p a (t m) -> p a m t", t=4),
                               in_=w8_raw[:].rearrange("p a (m t) -> p a m t", t=4))
-        nc.gpsimd.tensor_copy(out=w8s_dealt[:].rearrange("p (t m) -> p t m", t=4),
-                              in_=w8s_raw[:].rearrange("p (m t) -> p t m", t=4))
-        long1 = [late.tile([P, 4, JH], F32, name="long1_%d" % jh, offset=6144 * jh, align_bytes=64) for jh in range(2)]
+        long1 = [late.tile([P, 4, JH], F32, name="long1_%d" % jh, offset=6656 - 4096 * jh, align_bytes=64) for jh in range(2)]
 
         def pick_long(jh):
             for t in range(4):
                 nc.vector.tensor_copy(long1[jh][:, t, :], hs[4 + t][:].indirect(pos1_t[:, 16 * jh:16 * (jh + 1)]))
 
         pick_long(0)
+        nc.vector.tensor_copy(out=w8s_dealt[:].rearrange("p (t m) -> p t m", t=4),
+                              in_=w8s_raw[:].rearrange("p (m t) -> p t m", t=4))
         xbq = [quantize(xb_woven, "xbq0", 0), quantize(xb_woven1, "xbq1")]
         xaq = [quantize(xa_woven, "xaq0", 1)]
         waq = [quantize(wa_rounded[b], "waq%d" % b, 2 + b) for b in range(2)]
@@ -285,11 +274,11 @@ def tile_list_karyotype_arm_features_kernel(
         y_plane = tile([P, J], U8, "y_plane")
         out_rows = out_0.rearrange("(p t) j -> p t j", t=4)
         out_words = out_1[0].rearrange("p m i -> p (m i)").bitcast(I32)
+        xa_woven = tile([P, 2, 4 * JH], BF16, "xa_woven1", tag="xb_rows1")
         for jh in range(2):
             cols = slice(JH * jh, JH * (jh + 1))
-            xa_woven = tile([P, 4 * JH], BF16, "xa_woven1_%d" % jh)
-            nc.scalar.activation(out=weave_out(xa_woven[:]), in_=weave_in(long1[jh][:]), func=ACT.Abs)
-            nc.vector.quantize_mx(out=xa_codes[:, cols].bitcast(FP8X4), scales=xa_plane[:, cols], in_=xa_woven[:])
+            nc.scalar.activation(out=weave_out(xa_woven[:, jh, :]), in_=weave_in(long1[jh][:]), func=ACT.Abs)
+            nc.vector.quantize_mx(out=xa_codes[:, cols].bitcast(FP8X4), scales=xa_plane[:, cols], in_=xa_woven[:, jh, :])
         for jh in range(2):
             cols = slice(JH * jh, JH * (jh + 1))
             y = tile([P, 4, JH], F32, "y%d" % jh, tag="wa_raw%d" % jh)

@@ -40,32 +40,46 @@ def tile_list_karyotype_arm_features_kernel(
         def tile(shape, dtype, name, tag=None, bufs=1):
             return sb.tile(shape, dtype, name=name, tag=tag or name, bufs=bufs, align_bytes=64)
 
+        def late_tile(shape, dtype, name, offset):
+            return late.tile(shape, dtype, name=name, offset=offset, align_bytes=64)
+
         def zeroed_plane(width, name):
             plane = tile([P, width], U8, name)
             nc.vector.memset(plane[:].bitcast(I32), 0)
             return plane
 
+        def load_scale_rows(plane, row, scales):
+            rows = 4 * scales.shape[0]
+            for q in range(4):
+                nc.sync.dma_start(out=plane[32 * q + row:32 * q + row + rows, :].bitcast(I32),
+                                  in_=scales[:, 4 * q:4 * q + 4, :].bitcast(I32))
+
+        def move_scale_rows(dst, src):
+            for q in range(4):
+                nc.sync.dma_start(out=dst[32 * q:32 * q + 4, :].bitcast(I32),
+                                  in_=src[32 * q + 4:32 * q + 8, :].bitcast(I32))
+
         offs_t = lists.tile([P, S // 16], U16, name="offs_t")
         pos1_t = lists.tile([P, J // 16], U16, name="pos1_t")
         pos2_t = lists.tile([P, J // 16], U16, name="pos2_t")
 
+        w4s_raw = zeroed_plane(H, "w4s_raw")
         tabs = zeroed_plane(T, "tabs")
-        w4s_raw = zeroed_plane(2 * H, "w4s_raw")
         gs2 = zeroed_plane(S, "gs2")
+        w4s_moved = zeroed_plane(H, "w4s_moved")
         w8s_raw = zeroed_plane(N, "w8s_raw")
 
         tabw = [tile([P, T], U32, "tabw%d" % a) for a in range(3)]
         w1_raw = [tile([P, 4, 512], F32, "w1_raw%d" % b) for b in range(2)]
         wa_raw = [tile([P, 4, 512], F32, "wa_raw%d" % b) for b in range(2)]
         w4_raw = tile([P, 2, 2048], U8, "w4_raw")
-        stain_t = [tile([P, S], F32, "stain%d" % s) for s in range(7)]
-        stain_t.append(late.tile([P, S], F32, name="stain7", offset=0, align_bytes=64))
+        stain_t = [tile([P, 2, S], F32, "stain%d" % u) for u in range(3)]
+        stain_t.append(late_tile([P, 2, S], F32, "stain3", 0))
         gain_t = tile([P, 2, 4], F32, "gain_t")
-        gain_s = tile([P, 2, 4], F32, "gain_s", tag="xb_rows0")
         shift_t = tile([P, 2, 4], F32, "shift_t")
         w8_raw = tile([P, 2, N], I32, "w8_raw")
         res_t = tile([P, 4, J], F32, "res_t")
-        stain_rows = stain.rearrange("(b p t) m -> b t p m", b=2, t=4)
+        stain_rows = stain.rearrange("(b p u e) m -> b u p e m", b=2, u=2, e=2)
 
         def load_tab(a):
             nc.sync.dma_start(out=tabw[a][:].bitcast(I32),
@@ -79,27 +93,17 @@ def tile_list_karyotype_arm_features_kernel(
             nc.sync.dma_start(out=wa_raw[b][:],
                               in_=wa[512 * b:512 * (b + 1), :].rearrange("(p j) c -> p j c", j=4))
 
-        def load_stain(s):
-            nc.sync.dma_start(out=stain_t[s][:], in_=stain_rows[s // 4, s % 4])
-
-        def load_tab_scales(passes, row):
-            for q in range(4):
-                rows = slice(32 * q + row, 32 * q + row + 4 * len(passes))
-                nc.sync.dma_start(out=tabs[rows, :].bitcast(I32),
-                                  in_=tab_scales[passes.start:passes.stop, 4 * q:4 * q + 4, :].bitcast(I32))
+        def load_stain(u):
+            nc.sync.dma_start(out=stain_t[u][:], in_=stain_rows[u // 2, u % 2])
 
         nc.sync.dma_start(offs_t[:], offs)
         load_tab(0)
-        load_tab_scales(range(1, 3), 0)
+        load_scale_rows(w4s_raw, 0, w4_scales)
         load_tab(1)
-        load_tab_scales(range(0, 1), 8)
+        load_scale_rows(tabs, 0, tab_scales[1:3])
         load_w1(0)
-        for q in range(4):
-            nc.sync.dma_start(
-                out=w4s_raw[32 * q:32 * q + 4, :].bitcast(I32).rearrange("r (a c) -> r a c", a=2),
-                in_=w4_scales[:, 4 * q:4 * q + 4, :].bitcast(I32).rearrange("a r c -> r a c"))
+        load_scale_rows(tabs, 8, tab_scales[0:1])
         nc.sync.dma_start(out=w4_raw[:].bitcast(I32), in_=w4_words.rearrange("a p c -> p a c").bitcast(I32))
-        load_w1(1)
         load_tab(2)
 
         gw = [tile([P, S], U32, "gw%d" % a) for a in range(3)]
@@ -107,32 +111,24 @@ def tile_list_karyotype_arm_features_kernel(
         nc.vector.tensor_copy(gw[0][:], tabw[0][:].indirect(offs_t[:]))
         nc.vector.tensor_copy(gs[:], tabs[:].indirect(offs_t[:]))
         nc.vector.tensor_copy(gw[1][:], tabw[1][:].indirect(offs_t[:]))
-        for q in range(4):
-            nc.sync.dma_start(out=gs2[32 * q:32 * q + 4, :].bitcast(I32),
-                              in_=gs[32 * q + 4:32 * q + 8, :].bitcast(I32))
-
-        load_wa(0)
-        nc.sync.dma_start(out=gain_t[:], in_=gain.rearrange("(b p t) -> p b t", b=2, t=4))
-        nc.sync.dma_start(out=gain_s[:], in_=gain.rearrange("(b p t) -> p b t", b=2, t=4))
-        nc.sync.dma_start(pos2_t[:], pos2)
+        w4s_dealt = tile([P, H], U8, "w4s_dealt")
+        nc.vector.tensor_copy(out=w4s_dealt[:].rearrange("p (b t m) -> p b t m", b=2, t=4),
+                              in_=w4s_raw[:].rearrange("p (b m t) -> p b t m", b=2, t=4))
+        move_scale_rows(w4s_moved, w4s_dealt)
         load_stain(0)
+        move_scale_rows(gs2, gs)
+        nc.sync.dma_start(out=gain_t[:], in_=gain.rearrange("(b p t) -> p b t", b=2, t=4))
+        nc.sync.dma_start(pos2_t[:], pos2)
         nc.sync.dma_start(pos1_t[:], pos1)
-        for x in (1, 2, "shift", 3, 4, 5, "wa1", 6, 7, "w8"):
-            if x == "w1":
-                load_w1(1)
-            elif x == "wa0":
-                load_wa(0)
-            elif x == "wa1":
-                load_wa(1)
-            elif x == "shift":
-                nc.sync.dma_start(out=shift_t[:], in_=shift.rearrange("(b p t) -> p b t", b=2, t=4))
-            elif x == "w8":
-                nc.sync.dma_start(out=w8_raw[:], in_=w8_words.rearrange("a p c i -> p a (c i)").bitcast(I32))
-                for q in range(4):
-                    nc.sync.dma_start(out=w8s_raw[32 * q:32 * q + 8, :].bitcast(I32),
-                                      in_=w8_scales[:, 4 * q:4 * q + 4, :].bitcast(I32))
-            else:
-                load_stain(x)
+        load_w1(1)
+        nc.sync.dma_start(out=shift_t[:], in_=shift.rearrange("(b p t) -> p b t", b=2, t=4))
+        load_stain(1)
+        load_wa(0)
+        load_stain(2)
+        load_wa(1)
+        nc.sync.dma_start(out=w8_raw[:], in_=w8_words.rearrange("a p c i -> p a (c i)").bitcast(I32))
+        load_scale_rows(w8s_raw, 0, w8_scales)
+        load_stain(3)
         nc.sync.dma_start(out=res_t[:], in_=res.rearrange("(p t) j -> p t j", t=4))
 
         def round_weight(raw, name):
@@ -146,54 +142,48 @@ def tile_list_karyotype_arm_features_kernel(
             if place is None:
                 plane = tile([P, 512], U8, name + "_plane")
             else:
-                plane = late.tile([P, 512], U8, name=name + "_plane", offset=512 * place, align_bytes=64)
+                plane = late_tile([P, 512], U8, name + "_plane", 512 * place)
             nc.vector.quantize_mx(out=codes[:].bitcast(FP8X4), scales=plane[:], in_=rounded[:])
             return codes, plane
 
-        w4s_dealt = tile([P, 4, 512], U8, "w4s_dealt")
-        nc.vector.tensor_copy(out=w4s_dealt[:].rearrange("p g (t m) -> p g t m", t=4),
-                              in_=w4s_raw[:].rearrange("p (g m t) -> p g t m", g=4, t=4))
         w4_dealt = tile([P, 4, 1024], U8, "w4_dealt")
         nc.vector.tensor_copy(
             out=w4_dealt[:].bitcast(U16).rearrange("p g (t m) -> p g t m", t=4),
             in_=w4_raw[:].bitcast(U16).rearrange("p a (b m t) -> p (a b) t m", b=2, t=4))
-        w1q = [quantize(round_weight(w1_raw[b], "w1_rounded%d" % b), "w1q%d" % b) for b in range(2)]
+        w1q = [quantize(round_weight(w1_raw[0], "w1_rounded0"), "w1q0")]
         nc.vector.tensor_copy(gw[2][:, 0:512], tabw[2][:].indirect(offs_t[:, 0:32]))
         nc.vector.tensor_copy(gw[2][:, 512:1024], tabw[2][:].indirect(offs_t[:, 32:64]))
+        w1_rounded1 = round_weight(w1_raw[1], "w1_rounded1")
+        wa_rounded = [round_weight(wa_raw[b], "wa_rounded%d" % b) for b in range(2)]
 
         moving_planes = [gs[8:P, :], gs[:], gs2[:]]
 
         def make_h(s):
             b, t = divmod(s, 4)
-            h = tile([P, S], F32, "h%d" % s)
-            cols = slice(128 * t, 128 * (t + 1))
-            order = (0, 1, 2) if s in (0, 2) else (2, 0, 1)
+            h = tile([P, S], F32, "h%d" % s, tag="h", bufs=6)
+            n0 = 128 * t
+            order = (0, 1, 2) if s == 0 else (2, 0, 1)
             for half in range(2):
                 m = slice(BANK * half, BANK * (half + 1))
                 bank = psum.tile([P, BANK], F32, name="raw_bank", tag="bank")
                 for a in order:
                     if a == 0:
-                        codes, plane = w1q[b][0][:, cols].bitcast(FP8X4), w1q[b][1][:, cols]
+                        codes, plane = w1q[b][0][:, n0:n0 + 128].bitcast(FP8X4), w1q[b][1][:, n0:n0 + 128]
                     else:
-                        codes = w4_dealt[:, 2 * (a - 1) + b, 256 * t:256 * (t + 1)].bitcast(FP4X4)
-                        plane = w4s_dealt[:, 2 * (a - 1) + b, cols]
+                        codes = w4_dealt[:, 2 * (a - 1) + b, 2 * n0:2 * n0 + 256].bitcast(FP4X4)
+                        plane = (w4s_dealt, w4s_moved)[a - 1][:, 512 * b + n0:512 * b + n0 + 128]
                     nc.tensor.matmul_mx(
                         out=bank[:], lhsT=codes, lhsT_scale=plane,
                         rhs=gw[a][:, m].bitcast(FP8X4), rhs_scale=moving_planes[a][:, m],
                         start=(a == order[0]), stop=(a == order[-1]))
-                if (s, half) in ((0, 0), (0, 1), (1, 0), (1, 1), (4, 0), (4, 1)):
-                    nc.vector.scalar_tensor_tensor(
-                        out=h[:, m], in0=bank[:], scalar=gain_t[:, b, t:t + 1], in1=stain_t[s][:, m],
-                        op0=MULT, op1=MULT)
-                else:
-                    nc.scalar.activation(out=h[:, m], in_=bank[:], func=ACT.Copy, scale=(gain_s if s <= 5 else gain_t)[:, b, t:t + 1])
-                    for c0 in range(m.start, m.stop, 512):
-                        c = slice(c0, c0 + 512)
-                        nc.gpsimd.tensor_tensor(out=h[:, c], in0=h[:, c], in1=stain_t[s][:, c], op=MULT)
+                nc.vector.scalar_tensor_tensor(
+                    out=h[:, m], in0=bank[:], scalar=gain_t[:, b, t:t + 1], in1=stain_t[s // 2][:, s % 2, m],
+                    op0=MULT, op1=MULT)
             return h
 
-        def short_arm(h, b, t, rows, tag, bufs):
-            picked = tile([P, J], F32, "picked2_%d" % (4 * b + t), tag=tag, bufs=bufs)
+        def short_arm(h, s, rows):
+            b, t = divmod(s, 4)
+            picked = tile([P, J], F32, "picked2_%d" % s, tag="picked2", bufs=6)
             nc.vector.tensor_copy(picked[:], h[:].indirect(pos2_t[:]))
             nc.scalar.activation(out=rows[:, t, :], in_=picked[:], func=ACT.Identity,
                                  bias=shift_t[:, b, t:t + 1])
@@ -204,43 +194,43 @@ def tile_list_karyotype_arm_features_kernel(
         def weave_in(src):
             return src.rearrange("p t (c i) -> p c t i", i=4)
 
-        xb_rows = tile([P, 4, J], BF16, "xb_rows0")
+        xb_rows = tile([P, 4, J], BF16, "xb_rows0", tag="w1_raw1")
         long0 = tile([P, 4, J], F32, "long0", tag="w1_raw0")
-        hs = {s: make_h(s) for s in (0, 2, 1)}
-        for s in (3, 5, 4, 6, 7):
-            hs[s] = make_h(s)
-
-        wa_rounded = [round_weight(wa_raw[b], "wa_rounded%d" % b) for b in range(2)]
-        for t in range(4):
-            short_arm(hs[t], 0, t, xb_rows, "picked2", 6)
-            nc.vector.tensor_copy(long0[:, t, :], hs[t][:].indirect(pos1_t[:]))
-        xb_woven = tile([P, 2048], BF16, "xb_woven0", tag="rounded", bufs=5)
-        nc.scalar.copy(out=weave_out(xb_woven[:]), in_=weave_in(xb_rows[:]))
-        xa_woven = tile([P, 2048], BF16, "xa_woven0", tag="rounded", bufs=5)
-        nc.scalar.activation(out=weave_out(xa_woven[:]), in_=weave_in(long0[:]), func=ACT.Abs)
+        for pair in ((0, 1), (2, 3)):
+            hs = {t: make_h(t) for t in pair}
+            if pair[0] == 2:
+                w1q.append(quantize(w1_rounded1, "w1q1"))
+            for t in pair:
+                short_arm(hs[t], t, xb_rows)
+                nc.vector.tensor_copy(long0[:, t, :], hs[t][:].indirect(pos1_t[:]))
+        xb_woven0 = tile([P, 2048], BF16, "xb_woven0", tag="rounded", bufs=5)
+        nc.scalar.copy(out=weave_out(xb_woven0[:]), in_=weave_in(xb_rows[:]))
+        xa_woven0 = tile([P, 2048], BF16, "xa_woven0", tag="rounded", bufs=5)
+        nc.scalar.activation(out=weave_out(xa_woven0[:]), in_=weave_in(long0[:]), func=ACT.Abs)
 
         xb_rows = tile([P, 4, J], BF16, "xb_rows1")
-        for t in range(4):
-            short_arm(hs[4 + t], 1, t, xb_rows, "picked2", 6)
-        xb_woven1 = tile([P, 2048], BF16, "xb_woven1", tag="rounded", bufs=5)
+        long1 = [tile([P, 4, JH], F32, "long1_0"), late_tile([P, 4, JH], F32, "long1_1", 6656)]
+        hs = {}
+        for pair in ((0, 1), (2, 3)):
+            for t in pair:
+                hs[t] = make_h(4 + t)
+            for t in pair:
+                short_arm(hs[t], 4 + t, xb_rows)
+            for t in pair:
+                nc.vector.tensor_copy(long1[0][:, t, :], hs[t][:].indirect(pos1_t[:, 0:16]))
+        xb_woven1 = tile([P, 2048], BF16, "xb_woven1")
         nc.scalar.copy(out=weave_out(xb_woven1[:]), in_=weave_in(xb_rows[:]))
-        w8_dealt = tile([P, 2, N], I32, "w8_dealt")
-        w8s_dealt = late.tile([P, N], U8, name="w8s_dealt", offset=2048, align_bytes=64)
-        nc.gpsimd.tensor_copy(out=w8_dealt[:].rearrange("p a (t m) -> p a m t", t=4),
+        w8_dealt = late_tile([P, 2, N], I32, "w8_dealt", 2560)
+        w8s_dealt = late_tile([P, N], U8, "w8s_dealt", 2048)
+        nc.vector.tensor_copy(out=w8_dealt[:].rearrange("p a (t m) -> p a m t", t=4),
                               in_=w8_raw[:].rearrange("p a (m t) -> p a m t", t=4))
-        long1 = [late.tile([P, 4, JH], F32, name="long1_%d" % jh, offset=6656 - 4096 * jh, align_bytes=64) for jh in range(2)]
-
-        def pick_long(jh):
-            for t in range(4):
-                nc.vector.tensor_copy(long1[jh][:, t, :], hs[4 + t][:].indirect(pos1_t[:, 16 * jh:16 * (jh + 1)]))
-
-        pick_long(0)
         nc.vector.tensor_copy(out=w8s_dealt[:].rearrange("p (t m) -> p t m", t=4),
                               in_=w8s_raw[:].rearrange("p (m t) -> p t m", t=4))
-        xbq = [quantize(xb_woven, "xbq0", 0), quantize(xb_woven1, "xbq1")]
-        xaq = [quantize(xa_woven, "xaq0", 1)]
+        xbq = [quantize(xb_woven0, "xbq0", 0), quantize(xb_woven1, "xbq1")]
+        xaq = [quantize(xa_woven0, "xaq0", 1)]
         waq = [quantize(wa_rounded[b], "waq%d" % b, 2 + b) for b in range(2)]
-        pick_long(1)
+        for t in range(4):
+            nc.vector.tensor_copy(long1[1][:, t, :], hs[t][:].indirect(pos1_t[:, 16:32]))
         xa_codes = tile([P, 512], U32, "xaq1_codes")
         xa_plane = tile([P, 512], U8, "xaq1_plane")
         xaq.append((xa_codes, xa_plane))
@@ -263,7 +253,7 @@ def tile_list_karyotype_arm_features_kernel(
         def wa_cols(b, n):
             return waq[b][0][:, n], waq[b][1][:, n]
 
-        shifted = tile([P, 2, 4, JH], F32, "shifted", tag="w1_raw1")
+        shifted = tile([P, 2, 4, JH], F32, "shifted", tag="w1_raw0")
         for jh in range(2):
             for tp in range(2):
                 bank = second_stage(w8_cols, xbq, jh, tp)
@@ -274,11 +264,12 @@ def tile_list_karyotype_arm_features_kernel(
         y_plane = tile([P, J], U8, "y_plane")
         out_rows = out_0.rearrange("(p t) j -> p t j", t=4)
         out_words = out_1[0].rearrange("p m i -> p (m i)").bitcast(I32)
-        xa_woven = tile([P, 2, 4 * JH], BF16, "xa_woven1", tag="xb_rows1")
+        xa_woven1 = tile([P, 2, 4 * JH], BF16, "xa_woven1", tag="xb_rows1")
         for jh in range(2):
             cols = slice(JH * jh, JH * (jh + 1))
-            nc.scalar.activation(out=weave_out(xa_woven[:, jh, :]), in_=weave_in(long1[jh][:]), func=ACT.Abs)
-            nc.vector.quantize_mx(out=xa_codes[:, cols].bitcast(FP8X4), scales=xa_plane[:, cols], in_=xa_woven[:, jh, :])
+            nc.scalar.activation(out=weave_out(xa_woven1[:, jh, :]), in_=weave_in(long1[jh][:]), func=ACT.Abs)
+            nc.vector.quantize_mx(out=xa_codes[:, cols].bitcast(FP8X4), scales=xa_plane[:, cols],
+                                  in_=xa_woven1[:, jh, :])
         for jh in range(2):
             cols = slice(JH * jh, JH * (jh + 1))
             y = tile([P, 4, JH], F32, "y%d" % jh, tag="wa_raw%d" % jh)

@@ -20,10 +20,25 @@ S = 1024
 H = 1024
 N = 512
 J = 512
+PASS = 512
 BANK = 512
-JH = 256
+JH = J // 2
 
-FLOPS = 2 * 1536 * H * S + 2 * 2 * H * N * J
+VECTOR_SLICES = (0, 1, 4)
+LAST_SLICE_AHEAD_OF_SHIFTS = 5
+PICKED_BUFS = 6
+ROUNDED_BUFS = 4
+
+LATE_W8_WORDS = 0
+LATE_STAIN = 3584
+LATE_PLANES = 4096
+LATE_W8_PLANE = 5632
+LATE_LONG = 7168
+LAST_WA = 0
+LAST_XB_ROWS = 3072
+LAST_XA = 6144
+
+FLOPS = 2 * 3 * PASS * H * S + 2 * 2 * H * N * J
 
 
 def tile_list_karyotype_arm_features_kernel(
@@ -35,51 +50,49 @@ def tile_list_karyotype_arm_features_kernel(
         lists = ctx.enter_context(tc.tile_pool(name="lists", bufs=1))
         sb = ctx.enter_context(tc.tile_pool(name="sb", bufs=1))
         late = ctx.enter_context(tc.tile_pool(name="late", bufs=1))
+        last = ctx.enter_context(tc.tile_pool(name="last", bufs=1))
         psum = ctx.enter_context(tc.psum_pool(name="psum", bufs=8))
 
         def tile(shape, dtype, name, tag=None, bufs=1):
             return sb.tile(shape, dtype, name=name, tag=tag or name, bufs=bufs, align_bytes=64)
 
-        def late_tile(shape, dtype, name, offset):
-            return late.tile(shape, dtype, name=name, offset=offset, align_bytes=64)
+        def placed(pool, shape, dtype, name, offset):
+            return pool.tile(shape, dtype, name=name, offset=offset, align_bytes=64)
 
         def zeroed_plane(width, name):
             plane = tile([P, width], U8, name)
             nc.vector.memset(plane[:].bitcast(I32), 0)
             return plane
 
-        def load_scale_rows(plane, row, scales):
-            rows = 4 * scales.shape[0]
+        def load_two_passes_of_scales(plane, scales):
             for q in range(4):
-                nc.sync.dma_start(out=plane[32 * q + row:32 * q + row + rows, :].bitcast(I32),
+                nc.sync.dma_start(out=plane[32 * q:32 * q + 8, :].bitcast(I32),
                                   in_=scales[:, 4 * q:4 * q + 4, :].bitcast(I32))
 
-        def move_scale_rows(dst, src):
-            for q in range(4):
-                nc.sync.dma_start(out=dst[32 * q:32 * q + 4, :].bitcast(I32),
-                                  in_=src[32 * q + 4:32 * q + 8, :].bitcast(I32))
+        def load_by_slice(dst, vector):
+            nc.sync.dma_start(out=dst[:], in_=vector.rearrange("(b p t) -> p b t", b=2, t=4))
 
         offs_t = lists.tile([P, S // 16], U16, name="offs_t")
         pos1_t = lists.tile([P, J // 16], U16, name="pos1_t")
         pos2_t = lists.tile([P, J // 16], U16, name="pos2_t")
 
-        w4s_raw = zeroed_plane(H, "w4s_raw")
         tabs = zeroed_plane(T, "tabs")
+        w4s_raw = zeroed_plane(2 * H, "w4s_raw")
         gs2 = zeroed_plane(S, "gs2")
-        w4s_moved = zeroed_plane(H, "w4s_moved")
         w8s_raw = zeroed_plane(N, "w8s_raw")
 
         tabw = [tile([P, T], U32, "tabw%d" % a) for a in range(3)]
-        w1_raw = [tile([P, 4, 512], F32, "w1_raw%d" % b) for b in range(2)]
-        wa_raw = [tile([P, 4, 512], F32, "wa_raw%d" % b) for b in range(2)]
-        w4_raw = tile([P, 2, 2048], U8, "w4_raw")
-        stain_t = [tile([P, 2, S], F32, "stain%d" % u) for u in range(3)]
-        stain_t.append(late_tile([P, 2, S], F32, "stain3", 0))
+        w1_raw = [tile([P, 4, PASS], F32, "w1_raw%d" % b) for b in range(2)]
+        wa_raw = [tile([P, 4, N], F32, "wa_raw%d" % b) for b in range(2)]
+        w4_raw = [tile([P, 2, 2 * PASS], U8, "w4_raw%d" % b) for b in range(2)]
+        stain_t = [tile([P, S], F32, "stain%d" % s) for s in range(7)]
+        stain_t.append(placed(late, [P, S], F32, "stain7", LATE_STAIN))
+        gain_first = tile([P, 2, 4], F32, "gain_s", tag="xb_rows0")
         gain_t = tile([P, 2, 4], F32, "gain_t")
         shift_t = tile([P, 2, 4], F32, "shift_t")
         w8_raw = tile([P, 2, N], I32, "w8_raw")
         res_t = tile([P, 4, J], F32, "res_t")
-        stain_rows = stain.rearrange("(b p u e) m -> b u p e m", b=2, u=2, e=2)
+        stain_rows = stain.rearrange("(b p t) m -> b t p m", b=2, t=4)
 
         def load_tab(a):
             nc.sync.dma_start(out=tabw[a][:].bitcast(I32),
@@ -87,23 +100,31 @@ def tile_list_karyotype_arm_features_kernel(
 
         def load_w1(b):
             nc.sync.dma_start(out=w1_raw[b][:],
-                              in_=w1[:, 512 * b:512 * (b + 1)].rearrange("(p j) c -> p j c", j=4))
+                              in_=w1[:, PASS * b:PASS * (b + 1)].rearrange("(p i) c -> p i c", i=4))
+
+        def load_w4(b):
+            columns = w4_words[:, :, 2 * PASS * b:2 * PASS * (b + 1)]
+            nc.sync.dma_start(out=w4_raw[b][:].bitcast(I32), in_=columns.rearrange("a p c -> p a c").bitcast(I32))
 
         def load_wa(b):
             nc.sync.dma_start(out=wa_raw[b][:],
-                              in_=wa[512 * b:512 * (b + 1), :].rearrange("(p j) c -> p j c", j=4))
+                              in_=wa[PASS * b:PASS * (b + 1), :].rearrange("(p i) c -> p i c", i=4))
 
-        def load_stain(u):
-            nc.sync.dma_start(out=stain_t[u][:], in_=stain_rows[u // 2, u % 2])
+        def load_stain(s):
+            nc.sync.dma_start(out=stain_t[s][:], in_=stain_rows[s // 4, s % 4])
 
         nc.sync.dma_start(offs_t[:], offs)
         load_tab(0)
-        load_scale_rows(w4s_raw, 0, w4_scales)
         load_tab(1)
-        load_scale_rows(tabs, 0, tab_scales[1:3])
+        load_two_passes_of_scales(tabs, tab_scales[1:3])
+        for r in range(4):
+            nc.gpsimd.dma_start(out=tabs[8 + r:P:32, :].bitcast(I32), in_=tab_scales[0, r:16:4, :].bitcast(I32))
         load_w1(0)
-        load_scale_rows(tabs, 8, tab_scales[0:1])
-        nc.sync.dma_start(out=w4_raw[:].bitcast(I32), in_=w4_words.rearrange("a p c -> p a c").bitcast(I32))
+        for r in range(4):
+            nc.sync.dma_start(
+                out=w4s_raw[r:P:32, :].bitcast(I32).rearrange("q (a c) -> q a c", a=2),
+                in_=w4_scales[:, r:16:4, :].bitcast(I32).rearrange("a q c -> q a c"))
+        load_w4(0)
         load_tab(2)
 
         gw = [tile([P, S], U32, "gw%d" % a) for a in range(3)]
@@ -111,79 +132,100 @@ def tile_list_karyotype_arm_features_kernel(
         nc.vector.tensor_copy(gw[0][:], tabw[0][:].indirect(offs_t[:]))
         nc.vector.tensor_copy(gs[:], tabs[:].indirect(offs_t[:]))
         nc.vector.tensor_copy(gw[1][:], tabw[1][:].indirect(offs_t[:]))
-        w4s_dealt = tile([P, H], U8, "w4s_dealt")
-        nc.vector.tensor_copy(out=w4s_dealt[:].rearrange("p (b t m) -> p b t m", b=2, t=4),
-                              in_=w4s_raw[:].rearrange("p (b m t) -> p b t m", b=2, t=4))
-        move_scale_rows(w4s_moved, w4s_dealt)
+
+        def deal_w4_scales(b, tag):
+            plane = tile([P, 2, PASS], U8, "w4s_dealt%d" % b, tag=tag)
+            nc.vector.tensor_copy(out=plane[:].rearrange("p a (t m) -> p a t m", t=4),
+                                  in_=w4s_raw[:].rearrange("p (a b m t) -> p b a t m", a=2, b=2, t=4)[:, b])
+            return plane
+
+        w4s_dealt = [deal_w4_scales(0, "w4s_dealt0")]
         load_stain(0)
-        move_scale_rows(gs2, gs)
-        nc.sync.dma_start(out=gain_t[:], in_=gain.rearrange("(b p t) -> p b t", b=2, t=4))
-        nc.sync.dma_start(pos2_t[:], pos2)
-        nc.sync.dma_start(pos1_t[:], pos1)
+        load_by_slice(gain_t, gain)
+        for r in range(4):
+            nc.sync.dma_start(out=gs2[r:P:32, :].bitcast(I32), in_=gs[4 + r:P:32, :].bitcast(I32))
         load_w1(1)
-        nc.sync.dma_start(out=shift_t[:], in_=shift.rearrange("(b p t) -> p b t", b=2, t=4))
+        load_by_slice(gain_first, gain)
+        nc.sync.dma_start(pos2_t[:], pos2)
+        load_w4(1)
         load_stain(1)
-        load_wa(0)
+        nc.sync.dma_start(pos1_t[:], pos1)
         load_stain(2)
-        load_wa(1)
+        load_by_slice(shift_t, shift)
+        for s in range(3, 6):
+            load_stain(s)
+        load_wa(0)
+        for s in range(6, 8):
+            load_stain(s)
         nc.sync.dma_start(out=w8_raw[:], in_=w8_words.rearrange("a p c i -> p a (c i)").bitcast(I32))
-        load_scale_rows(w8s_raw, 0, w8_scales)
-        load_stain(3)
+        load_two_passes_of_scales(w8s_raw, w8_scales)
+        load_wa(1)
         nc.sync.dma_start(out=res_t[:], in_=res.rearrange("(p t) j -> p t j", t=4))
 
-        def round_weight(raw, name):
-            rounded = tile([P, 2048], BF16, name, tag="rounded", bufs=5)
-            nc.scalar.copy(out=rounded[:].rearrange("p (t m j) -> p m j t", t=4, j=4),
-                           in_=raw[:].rearrange("p j (m t) -> p m j t", t=4))
+        def rounded_tile(name):
+            return tile([P, 4 * PASS], BF16, name, tag="rounded", bufs=ROUNDED_BUFS)
+
+        def round_weight(raw, rounded):
+            nc.scalar.copy(out=rounded[:].rearrange("p (t m i) -> p m i t", t=4, i=4),
+                           in_=raw[:].rearrange("p i (m t) -> p m i t", t=4))
             return rounded
 
-        def quantize(rounded, name, place=None):
-            codes = tile([P, 512], U32, name + "_codes")
-            if place is None:
-                plane = tile([P, 512], U8, name + "_plane")
+        def quantize(woven, name, late_plane=None):
+            codes = tile([P, PASS], U32, name + "_codes")
+            if late_plane is None:
+                plane = tile([P, PASS], U8, name + "_plane")
             else:
-                plane = late_tile([P, 512], U8, name + "_plane", 512 * place)
-            nc.vector.quantize_mx(out=codes[:].bitcast(FP8X4), scales=plane[:], in_=rounded[:])
+                plane = placed(late, [P, PASS], U8, name + "_plane", LATE_PLANES + PASS * late_plane)
+            nc.vector.quantize_mx(out=codes[:].bitcast(FP8X4), scales=plane[:], in_=woven[:])
             return codes, plane
 
-        w4_dealt = tile([P, 4, 1024], U8, "w4_dealt")
-        nc.vector.tensor_copy(
-            out=w4_dealt[:].bitcast(U16).rearrange("p g (t m) -> p g t m", t=4),
-            in_=w4_raw[:].bitcast(U16).rearrange("p a (b m t) -> p (a b) t m", b=2, t=4))
-        w1q = [quantize(round_weight(w1_raw[0], "w1_rounded0"), "w1q0")]
-        nc.vector.tensor_copy(gw[2][:, 0:512], tabw[2][:].indirect(offs_t[:, 0:32]))
-        nc.vector.tensor_copy(gw[2][:, 512:1024], tabw[2][:].indirect(offs_t[:, 32:64]))
-        w1_rounded1 = round_weight(w1_raw[1], "w1_rounded1")
-        wa_rounded = [round_weight(wa_raw[b], "wa_rounded%d" % b) for b in range(2)]
+        def deal_w4(b):
+            words = tile([P, 2, 2 * PASS], U8, "w4_dealt%d" % b)
+            nc.vector.tensor_copy(
+                out=words[:].bitcast(U16).rearrange("p a (t m) -> p a t m", t=4),
+                in_=w4_raw[b][:].bitcast(U16).rearrange("p a (m t) -> p a t m", t=4))
+            return words
+
+        w4_dealt = [deal_w4(0)]
+        w1q = [quantize(round_weight(w1_raw[0], rounded_tile("w1_rounded0")), "w1q0")]
+        for m0 in range(0, S, BANK):
+            nc.vector.tensor_copy(gw[2][:, m0:m0 + BANK], tabw[2][:].indirect(offs_t[:, m0 // 16:(m0 + BANK) // 16]))
+        w4s_dealt.append(deal_w4_scales(1, "tabw2"))
+        w4_dealt.append(deal_w4(1))
 
         moving_planes = [gs[8:P, :], gs[:], gs2[:]]
 
         def make_h(s):
             b, t = divmod(s, 4)
-            h = tile([P, S], F32, "h%d" % s, tag="h", bufs=6)
-            n0 = 128 * t
+            h = tile([P, S], F32, "h%d" % s, tag="h", bufs=8)
+            n0 = P * t
             order = (0, 1, 2) if s == 0 else (2, 0, 1)
-            for half in range(2):
-                m = slice(BANK * half, BANK * (half + 1))
+            for m0 in range(0, S, BANK):
+                m = slice(m0, m0 + BANK)
                 bank = psum.tile([P, BANK], F32, name="raw_bank", tag="bank")
                 for a in order:
                     if a == 0:
-                        codes, plane = w1q[b][0][:, n0:n0 + 128].bitcast(FP8X4), w1q[b][1][:, n0:n0 + 128]
+                        codes, plane = w1q[b][0][:, n0:n0 + P].bitcast(FP8X4), w1q[b][1][:, n0:n0 + P]
                     else:
-                        codes = w4_dealt[:, 2 * (a - 1) + b, 2 * n0:2 * n0 + 256].bitcast(FP4X4)
-                        plane = (w4s_dealt, w4s_moved)[a - 1][:, 512 * b + n0:512 * b + n0 + 128]
+                        codes = w4_dealt[b][:, a - 1, 2 * n0:2 * (n0 + P)].bitcast(FP4X4)
+                        plane = w4s_dealt[b][:, a - 1, n0:n0 + P]
                     nc.tensor.matmul_mx(
                         out=bank[:], lhsT=codes, lhsT_scale=plane,
                         rhs=gw[a][:, m].bitcast(FP8X4), rhs_scale=moving_planes[a][:, m],
                         start=(a == order[0]), stop=(a == order[-1]))
-                nc.vector.scalar_tensor_tensor(
-                    out=h[:, m], in0=bank[:], scalar=gain_t[:, b, t:t + 1], in1=stain_t[s // 2][:, s % 2, m],
-                    op0=MULT, op1=MULT)
+                if s in VECTOR_SLICES:
+                    nc.vector.scalar_tensor_tensor(
+                        out=h[:, m], in0=bank[:], scalar=gain_t[:, b, t:t + 1], in1=stain_t[s][:, m],
+                        op0=MULT, op1=MULT)
+                else:
+                    gains = gain_first if s <= LAST_SLICE_AHEAD_OF_SHIFTS else gain_t
+                    nc.scalar.activation(out=h[:, m], in_=bank[:], func=ACT.Copy, scale=gains[:, b, t:t + 1])
+                    nc.gpsimd.tensor_tensor(out=h[:, m], in0=h[:, m], in1=stain_t[s][:, m], op=MULT)
             return h
 
         def short_arm(h, s, rows):
             b, t = divmod(s, 4)
-            picked = tile([P, J], F32, "picked2_%d" % s, tag="picked2", bufs=6)
+            picked = tile([P, J], F32, "picked2_%d" % s, tag="picked2", bufs=PICKED_BUFS)
             nc.vector.tensor_copy(picked[:], h[:].indirect(pos2_t[:]))
             nc.scalar.activation(out=rows[:, t, :], in_=picked[:], func=ACT.Identity,
                                  bias=shift_t[:, b, t:t + 1])
@@ -194,45 +236,52 @@ def tile_list_karyotype_arm_features_kernel(
         def weave_in(src):
             return src.rearrange("p t (c i) -> p c t i", i=4)
 
-        xb_rows = tile([P, 4, J], BF16, "xb_rows0", tag="w1_raw1")
+        hs = {s: make_h(s) for s in (0, 1)}
+        w1q.append(quantize(round_weight(w1_raw[1], rounded_tile("w1_rounded1")), "w1q1"))
+        for s in (2, 3, 5, 4, 6, 7):
+            hs[s] = make_h(s)
+
+        wa_rounded0 = round_weight(wa_raw[0], rounded_tile("wa_rounded0"))
+        xb_rows0 = tile([P, 4, J], BF16, "xb_rows0")
         long0 = tile([P, 4, J], F32, "long0", tag="w1_raw0")
-        for pair in ((0, 1), (2, 3)):
-            hs = {t: make_h(t) for t in pair}
-            if pair[0] == 2:
-                w1q.append(quantize(w1_rounded1, "w1q1"))
-            for t in pair:
-                short_arm(hs[t], t, xb_rows)
-                nc.vector.tensor_copy(long0[:, t, :], hs[t][:].indirect(pos1_t[:]))
-        xb_woven0 = tile([P, 2048], BF16, "xb_woven0", tag="rounded", bufs=5)
-        nc.scalar.copy(out=weave_out(xb_woven0[:]), in_=weave_in(xb_rows[:]))
-        xa_woven0 = tile([P, 2048], BF16, "xa_woven0", tag="rounded", bufs=5)
+        for t in range(4):
+            short_arm(hs[t], t, xb_rows0)
+            nc.vector.tensor_copy(long0[:, t, :], hs[t][:].indirect(pos1_t[:]))
+        xb_woven0 = tile([P, 4 * J], BF16, "xb_woven0", tag="stain6")
+        nc.gpsimd.tensor_scalar(out=xb_woven0[:].rearrange("p (j t) -> p j t", t=4),
+                                in0=xb_rows0[:].rearrange("p t j -> p j t"),
+                                scalar1=1.0, scalar2=0.0, op0=MULT, op1=ADD)
+
+        xa_woven0 = rounded_tile("xa_woven0")
         nc.scalar.activation(out=weave_out(xa_woven0[:]), in_=weave_in(long0[:]), func=ACT.Abs)
 
-        xb_rows = tile([P, 4, J], BF16, "xb_rows1")
-        long1 = [tile([P, 4, JH], F32, "long1_0"), late_tile([P, 4, JH], F32, "long1_1", 6656)]
-        hs = {}
-        for pair in ((0, 1), (2, 3)):
-            for t in pair:
-                hs[t] = make_h(4 + t)
-            for t in pair:
-                short_arm(hs[t], 4 + t, xb_rows)
-            for t in pair:
-                nc.vector.tensor_copy(long1[0][:, t, :], hs[t][:].indirect(pos1_t[:, 0:16]))
-        xb_woven1 = tile([P, 2048], BF16, "xb_woven1")
-        nc.scalar.copy(out=weave_out(xb_woven1[:]), in_=weave_in(xb_rows[:]))
-        w8_dealt = late_tile([P, 2, N], I32, "w8_dealt", 2560)
-        w8s_dealt = late_tile([P, N], U8, "w8s_dealt", 2048)
-        nc.vector.tensor_copy(out=w8_dealt[:].rearrange("p a (t m) -> p a m t", t=4),
-                              in_=w8_raw[:].rearrange("p a (m t) -> p a m t", t=4))
+        xb_rows1 = placed(last, [P, 4, J], BF16, "xb_rows1", LAST_XB_ROWS)
+        long1 = [tile([P, 4, JH], F32, "long1_0"), placed(late, [P, 4, JH], F32, "long1_1", LATE_LONG)]
+
+        def long_arm_half(t, jh):
+            offsets = pos1_t[:, jh * JH // 16:(jh + 1) * JH // 16]
+            nc.vector.tensor_copy(long1[jh][:, t, :], hs[4 + t][:].indirect(offsets))
+
+        for t in range(4):
+            short_arm(hs[4 + t], 4 + t, xb_rows1)
+            long_arm_half(t, 0)
+        xb_woven1 = tile([P, 4 * J], BF16, "xb_woven1", tag="gw2")
+        nc.scalar.copy(out=weave_out(xb_woven1[:]), in_=weave_in(xb_rows1[:]))
+        w8_dealt = placed(late, [P, 2, N], I32, "w8_dealt", LATE_W8_WORDS)
+        w8s_dealt = placed(late, [P, N], U8, "w8s_dealt", LATE_W8_PLANE)
         nc.vector.tensor_copy(out=w8s_dealt[:].rearrange("p (t m) -> p t m", t=4),
                               in_=w8s_raw[:].rearrange("p (m t) -> p t m", t=4))
-        xbq = [quantize(xb_woven0, "xbq0", 0), quantize(xb_woven1, "xbq1")]
-        xaq = [quantize(xa_woven0, "xaq0", 1)]
-        waq = [quantize(wa_rounded[b], "waq%d" % b, 2 + b) for b in range(2)]
+        nc.vector.tensor_copy(out=w8_dealt[:].rearrange("p a (t m) -> p a m t", t=4),
+                              in_=w8_raw[:].rearrange("p a (m t) -> p a m t", t=4))
+        xbq = [quantize(xb_woven0, "xbq0", late_plane=0), quantize(xb_woven1, "xbq1")]
+        xaq = [quantize(xa_woven0, "xaq0", late_plane=2)]
+        waq = [quantize(wa_rounded0, "waq0", late_plane=1)]
         for t in range(4):
-            nc.vector.tensor_copy(long1[1][:, t, :], hs[t][:].indirect(pos1_t[:, 16:32]))
-        xa_codes = tile([P, 512], U32, "xaq1_codes")
-        xa_plane = tile([P, 512], U8, "xaq1_plane")
+            long_arm_half(t, 1)
+        wa_rounded1 = placed(last, [P, 4 * N], BF16, "wa_rounded1", LAST_WA)
+        waq.append(quantize(round_weight(wa_raw[1], wa_rounded1), "waq1"))
+        xa_codes = tile([P, J], U32, "xaq1_codes")
+        xa_plane = tile([P, J], U8, "xaq1_plane")
         xaq.append((xa_codes, xa_plane))
 
         def second_stage(stationary, moving, jh, tp):
@@ -240,7 +289,7 @@ def tile_list_karyotype_arm_features_kernel(
             cols = slice(JH * jh, JH * (jh + 1))
             for b in range(2):
                 for u in range(2):
-                    codes, plane = stationary(b, slice(128 * (2 * tp + u), 128 * (2 * tp + u + 1)))
+                    codes, plane = stationary(b, slice(P * (2 * tp + u), P * (2 * tp + u + 1)))
                     nc.tensor.matmul_mx(
                         out=bank[:, u, :], lhsT=codes.bitcast(FP8X4), lhsT_scale=plane,
                         rhs=moving[b][0][:, cols].bitcast(FP8X4), rhs_scale=moving[b][1][:, cols],
@@ -253,18 +302,18 @@ def tile_list_karyotype_arm_features_kernel(
         def wa_cols(b, n):
             return waq[b][0][:, n], waq[b][1][:, n]
 
-        shifted = tile([P, 2, 4, JH], F32, "shifted", tag="w1_raw0")
+        yb_res = tile([P, 2, 4, JH], F32, "shifted", tag="w1_raw1")
         for jh in range(2):
             for tp in range(2):
                 bank = second_stage(w8_cols, xbq, jh, tp)
-                nc.vector.tensor_tensor(out=shifted[:, jh, 2 * tp:2 * tp + 2, :], in0=bank[:],
+                nc.vector.tensor_tensor(out=yb_res[:, jh, 2 * tp:2 * tp + 2, :], in0=bank[:],
                                         in1=res_t[:, 2 * tp:2 * tp + 2, JH * jh:JH * (jh + 1)], op=ADD)
 
         y_codes = tile([P, J], U32, "y_codes")
         y_plane = tile([P, J], U8, "y_plane")
         out_rows = out_0.rearrange("(p t) j -> p t j", t=4)
         out_words = out_1[0].rearrange("p m i -> p (m i)").bitcast(I32)
-        xa_woven1 = tile([P, 2, 4 * JH], BF16, "xa_woven1", tag="xb_rows1")
+        xa_woven1 = placed(last, [P, 2, 4 * JH], BF16, "xa_woven1", LAST_XA)
         for jh in range(2):
             cols = slice(JH * jh, JH * (jh + 1))
             nc.scalar.activation(out=weave_out(xa_woven1[:, jh, :]), in_=weave_in(long1[jh][:]), func=ACT.Abs)
@@ -272,20 +321,19 @@ def tile_list_karyotype_arm_features_kernel(
                                   in_=xa_woven1[:, jh, :])
         for jh in range(2):
             cols = slice(JH * jh, JH * (jh + 1))
-            y = tile([P, 4, JH], F32, "y%d" % jh, tag="wa_raw%d" % jh)
+            y = tile([P, 4, JH], F32, "y%d" % jh, tag="stain%d" % jh)
             for tp in range(2):
                 bank = second_stage(wa_cols, xaq, jh, tp)
                 nc.vector.tensor_tensor(out=y[:, 2 * tp:2 * tp + 2, :], in0=bank[:],
-                                        in1=shifted[:, jh, 2 * tp:2 * tp + 2, :], op=MULT)
+                                        in1=yb_res[:, jh, 2 * tp:2 * tp + 2, :], op=MULT)
             nc.sync.dma_start(out=out_rows[:, :, cols], in_=y[:])
-            y_woven = tile([P, 4 * JH], BF16, "y_woven%d" % jh)
+            y_woven = tile([P, 4 * JH], BF16, "y_woven%d" % jh, tag="gw%d" % jh)
             if jh == 0:
                 nc.scalar.copy(out=weave_out(y_woven[:]), in_=weave_in(y[:]))
             else:
                 nc.vector.tensor_copy(out=weave_out(y_woven[:]), in_=weave_in(y[:]))
             nc.vector.quantize_mx(out=y_codes[:, cols].bitcast(FP8X4), scales=y_plane[:, cols], in_=y_woven[:])
-            nc.sync.dma_start(out=out_words[:, cols], in_=y_codes[:, cols].bitcast(I32))
-        for q in range(4):
-            queue = nc.sync if q % 2 == 0 else nc.scalar
-            queue.dma_start(out=out_2[0, 4 * q:4 * q + 4, :].bitcast(I32),
-                            in_=y_plane[32 * q:32 * q + 4, :].bitcast(I32))
+            nc.scalar.dma_start(out=out_words[:, cols], in_=y_codes[:, cols].bitcast(I32))
+        for r in range(4):
+            queue = nc.sync if r % 2 == 0 else nc.scalar
+            queue.dma_start(out=out_2[0, r:16:4, :].bitcast(I32), in_=y_plane[r:P:32, :].bitcast(I32))

from contextlib import ExitStack

import concourse.mybir as mybir

F32 = mybir.dt.float32
BF16 = mybir.dt.bfloat16
I32 = mybir.dt.int32
U32 = mybir.dt.uint32
U16 = mybir.dt.uint16
U8 = mybir.dt.uint8
FP8X4 = mybir.dt.float8_e4m3fn_x4
FP4X4 = mybir.dt.float4_e2m1fn_x4
MULT = mybir.AluOpType.mult
ADD = mybir.AluOpType.add
ACT = mybir.ActivationFunctionType

P = 128
T = 2048
S = 1024
H = 1024
N = 512
J = 512
PASS = 512
BANK = 512
JH = J // 2

VECTOR_SLICES = (0, 1, 4)
LAST_SLICE_AHEAD_OF_SHIFTS = 5
PICKED_BUFS = 6
ROUNDED_BUFS = 4

LATE_W8_WORDS = 0
LATE_STAIN = 3584
LATE_PLANES = 4096
LATE_W8_PLANE = 5632
LATE_LONG = 7168
LAST_WA = 0
LAST_XB_ROWS = 3072
LAST_XA = 6144

FLOPS = 2 * 3 * PASS * H * S + 2 * 2 * H * N * J


def tile_list_karyotype_arm_features_kernel(
    tc, tab_words, tab_scales, offs, pos1, pos2, w1, w4_words, w4_scales,
    stain, gain, shift, wa, w8_words, w8_scales, res, out_0, out_1, out_2,
):
    nc = tc.nc
    with ExitStack() as ctx:
        lists = ctx.enter_context(tc.tile_pool(name="lists", bufs=1))
        sb = ctx.enter_context(tc.tile_pool(name="sb", bufs=1))
        late = ctx.enter_context(tc.tile_pool(name="late", bufs=1))
        last = ctx.enter_context(tc.tile_pool(name="last", bufs=1))
        psum = ctx.enter_context(tc.psum_pool(name="psum", bufs=8))

        def tile(shape, dtype, name, tag=None, bufs=1):
            return sb.tile(shape, dtype, name=name, tag=tag or name, bufs=bufs, align_bytes=64)

        def placed(pool, shape, dtype, name, offset):
            return pool.tile(shape, dtype, name=name, offset=offset, align_bytes=64)

        def zeroed_plane(width, name):
            plane = tile([P, width], U8, name)
            nc.vector.memset(plane[:].bitcast(I32), 0)
            return plane

        def load_two_passes_of_scales(plane, scales):
            for q in range(4):
                nc.sync.dma_start(out=plane[32 * q:32 * q + 8, :].bitcast(I32),
                                  in_=scales[:, 4 * q:4 * q + 4, :].bitcast(I32))

        def load_by_slice(dst, vector):
            nc.sync.dma_start(out=dst[:], in_=vector.rearrange("(b p t) -> p b t", b=2, t=4))

        offs_t = lists.tile([P, S // 16], U16, name="offs_t")
        pos1_t = lists.tile([P, J // 16], U16, name="pos1_t")
        pos2_t = lists.tile([P, J // 16], U16, name="pos2_t")

        tabs = zeroed_plane(T, "tabs")
        w4s_raw = zeroed_plane(2 * H, "w4s_raw")
        gs2 = zeroed_plane(S, "gs2")
        w8s_raw = zeroed_plane(N, "w8s_raw")

        tabw = [tile([P, T], U32, "tabw%d" % a) for a in range(3)]
        w1_raw = [tile([P, 4, PASS], F32, "w1_raw%d" % b) for b in range(2)]
        wa_raw = [tile([P, 4, N], F32, "wa_raw%d" % b) for b in range(2)]
        w4_raw = [tile([P, 2, 2 * PASS], U8, "w4_raw%d" % b) for b in range(2)]
        stain_t = [tile([P, S], F32, "stain%d" % s) for s in range(7)]
        stain_t.append(placed(late, [P, S], F32, "stain7", LATE_STAIN))
        gain_first = tile([P, 2, 4], F32, "gain_s", tag="xb_rows0")
        gain_t = tile([P, 2, 4], F32, "gain_t")
        shift_t = tile([P, 2, 4], F32, "shift_t")
        w8_raw = tile([P, 2, N], I32, "w8_raw")
        res_t = tile([P, 4, J], F32, "res_t")
        stain_rows = stain.rearrange("(b p t) m -> b t p m", b=2, t=4)

        def load_tab(a):
            nc.sync.dma_start(out=tabw[a][:].bitcast(I32),
                              in_=tab_words[a].rearrange("p n i -> p (n i)").bitcast(I32))

        def load_w1(b):
            nc.sync.dma_start(out=w1_raw[b][:],
                              in_=w1[:, PASS * b:PASS * (b + 1)].rearrange("(p i) c -> p i c", i=4))

        def load_w4(b):
            columns = w4_words[:, :, 2 * PASS * b:2 * PASS * (b + 1)]
            nc.sync.dma_start(out=w4_raw[b][:].bitcast(I32), in_=columns.rearrange("a p c -> p a c").bitcast(I32))

        def load_wa(b):
            nc.sync.dma_start(out=wa_raw[b][:],
                              in_=wa[PASS * b:PASS * (b + 1), :].rearrange("(p i) c -> p i c", i=4))

        def load_stain(s):
            nc.sync.dma_start(out=stain_t[s][:], in_=stain_rows[s // 4, s % 4])

        nc.sync.dma_start(offs_t[:], offs)
        load_tab(0)
        load_tab(1)
        load_two_passes_of_scales(tabs, tab_scales[1:3])
        for r in range(4):
            nc.gpsimd.dma_start(out=tabs[8 + r:P:32, :].bitcast(I32), in_=tab_scales[0, r:16:4, :].bitcast(I32))
        load_w1(0)
        for r in range(4):
            nc.sync.dma_start(
                out=w4s_raw[r:P:32, :].bitcast(I32).rearrange("q (a c) -> q a c", a=2),
                in_=w4_scales[:, r:16:4, :].bitcast(I32).rearrange("a q c -> q a c"))
        load_w4(0)
        load_tab(2)

        gw = [tile([P, S], U32, "gw%d" % a) for a in range(3)]
        gs = tile([P, S], U8, "gs")
        nc.vector.tensor_copy(gw[0][:], tabw[0][:].indirect(offs_t[:]))
        nc.vector.tensor_copy(gs[:], tabs[:].indirect(offs_t[:]))
        nc.vector.tensor_copy(gw[1][:], tabw[1][:].indirect(offs_t[:]))

        def deal_w4_scales(b, tag):
            plane = tile([P, 2, PASS], U8, "w4s_dealt%d" % b, tag=tag)
            nc.vector.tensor_copy(out=plane[:].rearrange("p a (t m) -> p a t m", t=4),
                                  in_=w4s_raw[:].rearrange("p (a b m t) -> p b a t m", a=2, b=2, t=4)[:, b])
            return plane

        w4s_dealt = [deal_w4_scales(0, "w4s_dealt0")]
        load_stain(0)
        load_by_slice(gain_t, gain)
        for r in range(4):
            nc.sync.dma_start(out=gs2[r:P:32, :].bitcast(I32), in_=gs[4 + r:P:32, :].bitcast(I32))
        load_w1(1)
        load_by_slice(gain_first, gain)
        nc.sync.dma_start(pos2_t[:], pos2)
        load_w4(1)
        load_stain(1)
        nc.sync.dma_start(pos1_t[:], pos1)
        load_stain(2)
        load_by_slice(shift_t, shift)
        for s in range(3, 6):
            load_stain(s)
        load_wa(0)
        for s in range(6, 8):
            load_stain(s)
        nc.sync.dma_start(out=w8_raw[:], in_=w8_words.rearrange("a p c i -> p a (c i)").bitcast(I32))
        load_two_passes_of_scales(w8s_raw, w8_scales)
        load_wa(1)
        nc.sync.dma_start(out=res_t[:], in_=res.rearrange("(p t) j -> p t j", t=4))

        def rounded_tile(name):
            return tile([P, 4 * PASS], BF16, name, tag="rounded", bufs=ROUNDED_BUFS)

        def round_weight(raw, rounded):
            nc.scalar.copy(out=rounded[:].rearrange("p (t m i) -> p m i t", t=4, i=4),
                           in_=raw[:].rearrange("p i (m t) -> p m i t", t=4))
            return rounded

        def quantize(woven, name, late_plane=None):
            codes = tile([P, PASS], U32, name + "_codes")
            if late_plane is None:
                plane = tile([P, PASS], U8, name + "_plane")
            else:
                plane = placed(late, [P, PASS], U8, name + "_plane", LATE_PLANES + PASS * late_plane)
            nc.vector.quantize_mx(out=codes[:].bitcast(FP8X4), scales=plane[:], in_=woven[:])
            return codes, plane

        def deal_w4(b):
            words = tile([P, 2, 2 * PASS], U8, "w4_dealt%d" % b)
            nc.vector.tensor_copy(
                out=words[:].bitcast(U16).rearrange("p a (t m) -> p a t m", t=4),
                in_=w4_raw[b][:].bitcast(U16).rearrange("p a (m t) -> p a t m", t=4))
            return words

        w4_dealt = [deal_w4(0)]
        w1q = [quantize(round_weight(w1_raw[0], rounded_tile("w1_rounded0")), "w1q0")]
        for m0 in range(0, S, BANK):
            nc.vector.tensor_copy(gw[2][:, m0:m0 + BANK], tabw[2][:].indirect(offs_t[:, m0 // 16:(m0 + BANK) // 16]))
        w4s_dealt.append(deal_w4_scales(1, "tabw2"))
        w4_dealt.append(deal_w4(1))

        moving_planes = [gs[8:P, :], gs[:], gs2[:]]

        def make_h(s):
            b, t = divmod(s, 4)
            h = tile([P, S], F32, "h%d" % s, tag="h", bufs=8)
            n0 = P * t
            order = (0, 1, 2) if s == 0 else (2, 0, 1)
            for m0 in range(0, S, BANK):
                m = slice(m0, m0 + BANK)
                bank = psum.tile([P, BANK], F32, name="raw_bank", tag="bank")
                for a in order:
                    if a == 0:
                        codes, plane = w1q[b][0][:, n0:n0 + P].bitcast(FP8X4), w1q[b][1][:, n0:n0 + P]
                    else:
                        codes = w4_dealt[b][:, a - 1, 2 * n0:2 * (n0 + P)].bitcast(FP4X4)
                        plane = w4s_dealt[b][:, a - 1, n0:n0 + P]
                    nc.tensor.matmul_mx(
                        out=bank[:], lhsT=codes, lhsT_scale=plane,
                        rhs=gw[a][:, m].bitcast(FP8X4), rhs_scale=moving_planes[a][:, m],
                        start=(a == order[0]), stop=(a == order[-1]))
                if s in VECTOR_SLICES:
                    nc.vector.scalar_tensor_tensor(
                        out=h[:, m], in0=bank[:], scalar=gain_t[:, b, t:t + 1], in1=stain_t[s][:, m],
                        op0=MULT, op1=MULT)
                else:
                    gains = gain_first if s <= LAST_SLICE_AHEAD_OF_SHIFTS else gain_t
                    nc.scalar.activation(out=h[:, m], in_=bank[:], func=ACT.Copy, scale=gains[:, b, t:t + 1])
                    nc.gpsimd.tensor_tensor(out=h[:, m], in0=h[:, m], in1=stain_t[s][:, m], op=MULT)
            return h

        def short_arm(h, s, rows):
            b, t = divmod(s, 4)
            picked = tile([P, J], F32, "picked2_%d" % s, tag="picked2", bufs=PICKED_BUFS)
            nc.vector.tensor_copy(picked[:], h[:].indirect(pos2_t[:]))
            nc.scalar.activation(out=rows[:, t, :], in_=picked[:], func=ACT.Identity,
                                 bias=shift_t[:, b, t:t + 1])

        def weave_out(dst):
            return dst.rearrange("p (c i t) -> p c t i", i=4, t=4)

        def weave_in(src):
            return src.rearrange("p t (c i) -> p c t i", i=4)

        hs = {s: make_h(s) for s in (0, 1)}
        w1q.append(quantize(round_weight(w1_raw[1], rounded_tile("w1_rounded1")), "w1q1"))
        for s in (2, 3, 5, 4, 6, 7):
            hs[s] = make_h(s)

        wa_rounded0 = round_weight(wa_raw[0], rounded_tile("wa_rounded0"))
        xb_rows0 = tile([P, 4, J], BF16, "xb_rows0")
        long0 = tile([P, 4, J], F32, "long0", tag="w1_raw0")
        for t in range(4):
            short_arm(hs[t], t, xb_rows0)
            nc.vector.tensor_copy(long0[:, t, :], hs[t][:].indirect(pos1_t[:]))
        xb_woven0 = tile([P, 4 * J], BF16, "xb_woven0", tag="stain6")
        nc.gpsimd.tensor_scalar(out=xb_woven0[:].rearrange("p (j t) -> p j t", t=4),
                                in0=xb_rows0[:].rearrange("p t j -> p j t"),
                                scalar1=1.0, scalar2=0.0, op0=MULT, op1=ADD)

        xa_woven0 = rounded_tile("xa_woven0")
        nc.scalar.activation(out=weave_out(xa_woven0[:]), in_=weave_in(long0[:]), func=ACT.Abs)

        xb_rows1 = placed(last, [P, 4, J], BF16, "xb_rows1", LAST_XB_ROWS)
        long1 = [tile([P, 4, JH], F32, "long1_0"), placed(late, [P, 4, JH], F32, "long1_1", LATE_LONG)]

        def long_arm_half(t, jh):
            offsets = pos1_t[:, jh * JH // 16:(jh + 1) * JH // 16]
            nc.vector.tensor_copy(long1[jh][:, t, :], hs[4 + t][:].indirect(offsets))

        for t in range(4):
            short_arm(hs[4 + t], 4 + t, xb_rows1)
            long_arm_half(t, 0)
        xb_woven1 = tile([P, 4 * J], BF16, "xb_woven1", tag="gw2")
        nc.scalar.copy(out=weave_out(xb_woven1[:]), in_=weave_in(xb_rows1[:]))
        w8_dealt = placed(late, [P, 2, N], I32, "w8_dealt", LATE_W8_WORDS)
        w8s_dealt = placed(late, [P, N], U8, "w8s_dealt", LATE_W8_PLANE)
        nc.vector.tensor_copy(out=w8s_dealt[:].rearrange("p (t m) -> p t m", t=4),
                              in_=w8s_raw[:].rearrange("p (m t) -> p t m", t=4))
        nc.vector.tensor_copy(out=w8_dealt[:].rearrange("p a (t m) -> p a m t", t=4),
                              in_=w8_raw[:].rearrange("p a (m t) -> p a m t", t=4))
        xbq = [quantize(xb_woven0, "xbq0", late_plane=0), quantize(xb_woven1, "xbq1")]
        xaq = [quantize(xa_woven0, "xaq0", late_plane=2)]
        waq = [quantize(wa_rounded0, "waq0", late_plane=1)]
        for t in range(4):
            long_arm_half(t, 1)
        wa_rounded1 = placed(last, [P, 4 * N], BF16, "wa_rounded1", LAST_WA)
        waq.append(quantize(round_weight(wa_raw[1], wa_rounded1), "waq1"))
        xa_codes = tile([P, J], U32, "xaq1_codes")
        xa_plane = tile([P, J], U8, "xaq1_plane")
        xaq.append((xa_codes, xa_plane))

        def second_stage(stationary, moving, jh, tp):
            bank = psum.tile([P, 2, JH], F32, name="y_bank", tag="bank")
            cols = slice(JH * jh, JH * (jh + 1))
            for b in range(2):
                for u in range(2):
                    codes, plane = stationary(b, slice(P * (2 * tp + u), P * (2 * tp + u + 1)))
                    nc.tensor.matmul_mx(
                        out=bank[:, u, :], lhsT=codes.bitcast(FP8X4), lhsT_scale=plane,
                        rhs=moving[b][0][:, cols].bitcast(FP8X4), rhs_scale=moving[b][1][:, cols],
                        start=(b == 0 and u == 0), stop=(b == 1 and u == 1))
            return bank

        def w8_cols(b, n):
            return w8_dealt[:, b, n], w8s_dealt[4 * b:P, n]

        def wa_cols(b, n):
            return waq[b][0][:, n], waq[b][1][:, n]

        yb_res = tile([P, 2, 4, JH], F32, "shifted", tag="w1_raw1")
        for jh in range(2):
            for tp in range(2):
                bank = second_stage(w8_cols, xbq, jh, tp)
                nc.vector.tensor_tensor(out=yb_res[:, jh, 2 * tp:2 * tp + 2, :], in0=bank[:],
                                        in1=res_t[:, 2 * tp:2 * tp + 2, JH * jh:JH * (jh + 1)], op=ADD)

        y_codes = tile([P, J], U32, "y_codes")
        y_plane = tile([P, J], U8, "y_plane")
        out_rows = out_0.rearrange("(p t) j -> p t j", t=4)
        out_words = out_1[0].rearrange("p m i -> p (m i)").bitcast(I32)
        xa_woven1 = placed(last, [P, 2, 4 * JH], BF16, "xa_woven1", LAST_XA)
        for jh in range(2):
            cols = slice(JH * jh, JH * (jh + 1))
            nc.scalar.activation(out=weave_out(xa_woven1[:, jh, :]), in_=weave_in(long1[jh][:]), func=ACT.Abs)
            nc.vector.quantize_mx(out=xa_codes[:, cols].bitcast(FP8X4), scales=xa_plane[:, cols],
                                  in_=xa_woven1[:, jh, :])
        for jh in range(2):
            cols = slice(JH * jh, JH * (jh + 1))
            y = tile([P, 4, JH], F32, "y%d" % jh, tag="stain%d" % jh)
            for tp in range(2):
                bank = second_stage(wa_cols, xaq, jh, tp)
                nc.vector.tensor_tensor(out=y[:, 2 * tp:2 * tp + 2, :], in0=bank[:],
                                        in1=yb_res[:, jh, 2 * tp:2 * tp + 2, :], op=MULT)
            nc.sync.dma_start(out=out_rows[:, :, cols], in_=y[:])
            y_woven = tile([P, 4 * JH], BF16, "y_woven%d" % jh, tag="gw%d" % jh)
            if jh == 0:
                nc.scalar.copy(out=weave_out(y_woven[:]), in_=weave_in(y[:]))
            else:
                nc.vector.tensor_copy(out=weave_out(y_woven[:]), in_=weave_in(y[:]))
            nc.vector.quantize_mx(out=y_codes[:, cols].bitcast(FP8X4), scales=y_plane[:, cols], in_=y_woven[:])
            nc.scalar.dma_start(out=out_words[:, cols], in_=y_codes[:, cols].bitcast(I32))
        for r in range(4):
            queue = nc.sync if r % 2 == 0 else nc.scalar
            queue.dma_start(out=out_2[0, r:16:4, :].bitcast(I32), in_=y_plane[r:P:32, :].bitcast(I32))
